import numpy as np
import ml_dtypes


def mxq(x, axis, fmt="e4m3"):
    dtype, down = {"e4m3": (ml_dtypes.float8_e4m3fn, 7), "e5m2": (ml_dtypes.float8_e5m2, 14)}[fmt]
    v = np.moveaxis(np.asarray(x, np.float32).astype(ml_dtypes.bfloat16).astype(np.float64), axis, -1)
    blocks = v.reshape(v.shape[:-1] + (-1, 32))
    amax = np.abs(blocks).max(-1, keepdims=True)
    byte = np.maximum(np.where(amax > 0, np.frexp(amax)[1] - 1 + 127, 0) - down, 1)
    scale = np.exp2(byte - 127.0)
    codes = (blocks / scale).astype(np.float32).astype(dtype).astype(np.float64)
    return np.moveaxis((codes * scale).reshape(v.shape), -1, axis)


WIDE = False


def mx_kscale(k):
    if not WIDE:
        return np.ones(k)
    levels = np.array([10, -10, 5, -5, 0])
    if k % 512:
        return np.exp2(np.random.permutation(np.resize(levels, k // 32))).repeat(32)
    a = np.empty((k // 512, 16))
    for p in range(k // 512):
        a[p, :8] = np.random.permutation(np.resize(levels, 8))
        for g in range(8):
            far = levels[np.abs(levels - a[p, g]) >= 10]
            a[p, g + 8] = far[np.random.randint(len(far))]
    return np.exp2(a.ravel()).repeat(32)


def f64(x):
    return np.asarray(x).astype(np.float64)


def striped(idx):
    return np.tile(np.asarray(idx).reshape(-1, 16).T, (8, 1)).astype(np.uint16)


def unstriped(offs):
    return offs[:16].T.reshape(-1).astype(np.int64)


E2M1 = np.array([0.0, 0.5, 1.0, 1.5, 2.0, 3.0, 4.0, 6.0, -0.0, -0.5, -1.0, -1.5, -2.0, -3.0, -4.0, -6.0])


def pack_weight(w, fmt):
    k, n = w.shape
    w = f64(np.asarray(w, np.float32).astype(ml_dtypes.bfloat16)).reshape(k // 32, 32, n)
    amax = np.abs(w).max(1)
    if fmt == "e4m3":
        byte = np.frexp(amax)[1] - 1 + 127 - 7
    else:
        mant, ex = np.frexp(amax / 6.0)
        byte = np.where(mant > 0.5, ex, ex - 1) + 127
    byte = np.clip(np.where(amax > 0, byte, 1), 1, 254)
    scaled = (w * np.exp2(127.0 - byte)[:, None, :]).reshape(k, n).astype(np.float32)
    by_word = np.ascontiguousarray(scaled.reshape(k // 512, 128, 4, n).transpose(0, 1, 3, 2))
    if fmt == "e4m3":
        words = by_word.astype(ml_dtypes.float8_e4m3fn).view(np.uint8)
    else:
        c = by_word.astype(ml_dtypes.float4_e2m1fn).view(np.uint8) & 0xF
        words = (c[..., 0::2] | (c[..., 1::2] << 4)).reshape(k // 512, 128, 2 * n)
    return np.ascontiguousarray(words), np.ascontiguousarray(byte.astype(np.uint8).reshape(k // 512, 16, n))


def unpack_weight(words, scales, fmt):
    g, _, n = scales.shape
    words = np.ascontiguousarray(words).reshape(g, 128, n, -1)
    if fmt == "e4m3":
        vals = words.view(ml_dtypes.float8_e4m3fn).astype(np.float64)
    else:
        nib = np.empty((g, 128, n, 4), np.uint8)
        nib[..., 0::2] = words & 0xF
        nib[..., 1::2] = words >> 4
        vals = E2M1[nib]
    vals = vals * np.repeat(np.exp2(scales.astype(np.float64) - 127.0), 8, axis=1)[..., None]
    return vals.transpose(0, 1, 3, 2).reshape(g * 512, n)


def bf(x):
    return np.asarray(x, np.float32).astype(ml_dtypes.bfloat16)


def planes(Y):
    r, m = Y.shape
    b = f64(bf(Y)).reshape(r // 32, 32, m)
    amax = np.abs(b).max(1)
    byte = np.clip(np.where(amax > 0, np.frexp(amax)[1] - 1 + 127 - 7, 1), 1, 254)
    codes = (b * np.exp2(127.0 - byte)[:, None, :]).reshape(r, m).astype(np.float32).astype(ml_dtypes.float8_e4m3fn).view(np.uint8)
    words = codes.reshape(r // 512, 128, 4, m).transpose(0, 1, 3, 2)
    return np.ascontiguousarray(words), np.ascontiguousarray(byte.astype(np.uint8).reshape(r // 512, 16, m))


B, N, T, D, NQ = 1, 512, 2048, 512, 512


def setup_inputs():
    n = np.random.standard_normal
    idx = np.random.permutation(T)[:B * N]
    s = mx_kscale(D)[:, None]
    kp = pack_weight(n((D, T)) / s, "e4m3")
    return {
        "qT": (n((B, D, NQ)) * s * (1.00 / np.sqrt(D))).astype(np.float32),
        "k_words": kp[0],
        "k_scales": kp[1],
        "nb": np.tile(0.5 * n(2048), (128, 1)).astype(np.float32),
        "offs": striped(idx),
    }


def reference(qT, k_words, k_scales, nb, offs):
    idx = unstriped(offs)
    pick = lambda x, which: x[:, which].reshape(x.shape[0], B, -1).transpose(1, 0, 2)
    k = unpack_weight(k_words, k_scales, "e4m3")
    kg = pick(k, idx)
    qq = mxq(f64(qT), 1, "e4m3")
    a = kg.transpose(0, 2, 1) @ qq
    y = np.maximum(a + pick(f64(nb), idx)[:, :1, :].transpose(0, 2, 1), 0.0)
    Y = y[0]
    words, scales = planes(Y)
    return Y, words, scales

@@ -1,0 +1,148 @@
+from contextlib import ExitStack
+
+import concourse.mybir as mybir
+from concourse.masks import make_identity
+
+F32 = mybir.dt.float32
+BF16 = mybir.dt.bfloat16
+I32 = mybir.dt.int32
+U32 = mybir.dt.uint32
+U16 = mybir.dt.uint16
+U8 = mybir.dt.uint8
+FP8X4 = mybir.dt.float8_e4m3fn_x4
+RELU = mybir.ActivationFunctionType.Relu
+
+P = 128
+PACK = 4
+T = 2048
+N = 512
+NQ = 512
+D = 512
+LOAD = 256
+CHUNK = 128
+BIAS_ROW = P - 1
+ADD = mybir.AluOpType.add
+MAX = mybir.AluOpType.max
+
+FLOPS = 2 * N * NQ * D
+BYTES = D * NQ * 4 + P * T * 4 + 16 * T + T * 4 + P * 32 * 2 + N * NQ * 4 + N * NQ + 16 * NQ
+
+
+def woven(tile):
+    return tile.rearrange("p (c i t) -> p c t i", i=4, t=PACK)
+
+
+def planar(rows):
+    return rows.rearrange("p t (c i) -> p c t i", i=4)
+
+
+def tile_attend_plh_brelu_topk_kernel(tc, qT, k_words, k_scales, nb, offs, out_0, out_1, out_2):
+    nc = tc.nc
+    with ExitStack() as ctx:
+        sb = ctx.enter_context(tc.tile_pool(name="sb", bufs=1))
+        ps = ctx.enter_context(tc.psum_pool(name="ps", bufs=1))
+
+        offsets = sb.tile([P, N // 16], U16, name="offsets")
+        nc.sync.dma_start(offsets[:], offs)
+
+        ks = sb.tile([P, T], U8, name="ks", tag="scales_then_words", align_bytes=64)
+        nc.vector.memset(ks[:].bitcast(I32), 0)
+        for quad in range(4):
+            nc.scalar.dma_start(
+                ks[32 * quad : 32 * quad + 4, :].bitcast(I32),
+                k_scales[0, 4 * quad : 4 * quad + 4, :].bitcast(I32),
+            )
+        nbt = sb.tile([P, T], F32, name="nbt", tag="bias_then_queries")
+        nc.sync.dma_start(nbt[BIAS_ROW:P, :], nb[0:1, :])
+        nc.vector.memset(nbt[0:BIAS_ROW, :], 0.0)
+
+        kw = sb.tile([P, T], I32, name="kw", tag="words_then_codes", align_bytes=64)
+        nc.sync.dma_start(kw[:], k_words[0].rearrange("p t r -> p (t r)").bitcast(I32))
+
+        q_rows = qT[0].rearrange("(p j) q -> p j q", j=PACK)
+        q_raw0 = sb.tile([P, PACK, LOAD], F32, name="q_raw0")
+        nc.sync.dma_start(q_raw0[:], q_rows[:, :, 0:LOAD])
+
+        ident = sb.tile([P, P], F32, name="ident")
+        make_identity(nc, ident[:])
+
+        nbg = sb.tile([P, N], F32, name="nbg")
+        nc.vector.tensor_copy(nbg[:], nbt[:].indirect(offsets[:]))
+        q_raw1 = sb.tile([P, PACK, LOAD], F32, name="q_raw1", tag="bias_then_queries")
+        nc.sync.dma_start(q_raw1[:], q_rows[:, :, LOAD : 2 * LOAD])
+        q_raw = [q_raw0, q_raw1]
+
+        ksg = sb.tile([P, N], U8, name="ksg", align_bytes=64)
+        nc.vector.tensor_copy(ksg[:], ks[:].indirect(offsets[:]))
+        ksd = sb.tile([P, N], U8, name="ksd", align_bytes=64)
+        nc.vector.tensor_copy(
+            ksd[:].rearrange("p (r s) -> p s r", r=PACK),
+            ksg[:].rearrange("p (s r) -> p s r", r=PACK),
+        )
+        kg = sb.tile([P, N], U32, name="kg", tag="scales_then_words", align_bytes=64)
+        nc.vector.tensor_copy(
+            kg[:].rearrange("p (r s) -> p s r", r=PACK),
+            kw[:].bitcast(U32).indirect(offsets[:]),
+        )
+
+        bias_ps = ps.tile([P, PACK, P], F32, name="bias_ps", tag="bank7")
+        for r in range(PACK):
+            nc.tensor.transpose(bias_ps[:, r, :], nbg[:, r::PACK], ident[:])
+        bias = sb.tile([P, PACK], F32, name="bias")
+        nc.scalar.copy(bias[:], bias_ps[:, :, BIAS_ROW])
+
+        y_codes = sb.tile([P, NQ], I32, name="y_codes", align_bytes=64)
+        y_scales = sb.tile([P, NQ], U8, name="y_scales", align_bytes=64)
+        y_rows = out_0.rearrange("(p r) q -> p r q", r=PACK)
+        y_words = out_1[0].rearrange("p q u -> p (q u)").bitcast(I32)
+        q_codes = sb.tile([P, NQ], U32, name="q_codes", tag="words_then_codes", align_bytes=64)
+        q_scales = sb.tile([P, NQ], U8, name="q_scales", align_bytes=64)
+
+        n_chunks = NQ // CHUNK
+        last = n_chunks - 1
+        for c in range(n_chunks):
+            cols = slice(c * CHUNK, (c + 1) * CHUNK)
+            at = (c * CHUNK) % LOAD
+            src = planar(q_raw[c * CHUNK // LOAD][:, :, at : at + CHUNK])
+            q_bf = sb.tile([P, CHUNK * PACK], BF16, name=f"q_bf{c}", align_bytes=64)
+            if c == last:
+                nc.vector.tensor_copy(woven(q_bf[:]), src)
+            else:
+                nc.scalar.copy(woven(q_bf[:]), src)
+            nc.vector.quantize_mx(q_codes[:, cols].bitcast(FP8X4), q_scales[:, cols], q_bf[:])
+
+        for c in range(n_chunks):
+            cols = slice(c * CHUNK, (c + 1) * CHUNK)
+            y = sb.tile([P, PACK, CHUNK], F32, name=f"y{c}")
+            for h in range(2):
+                acc = ps.tile([P, 2, CHUNK], F32, name=f"acc{c}_{h}", tag=f"bank{2 * c + h}")
+                for u in range(2):
+                    r = 2 * h + u
+                    nc.tensor.matmul_mx(
+                        acc[:, u, :],
+                        lhsT=kg[:, r * P : (r + 1) * P].bitcast(FP8X4),
+                        lhsT_scale=ksd[:, r * P : (r + 1) * P],
+                        rhs=q_codes[:, cols].bitcast(FP8X4),
+                        rhs_scale=q_scales[:, cols],
+                        start=True,
+                        stop=True,
+                    )
+                for u in range(2):
+                    r = 2 * h + u
+                    if c == last and h == 1:
+                        nc.vector.tensor_scalar(y[:, r, :], acc[:, u, :], bias[:, r : r + 1], 0.0, ADD, MAX)
+                    else:
+                        nc.scalar.activation(y[:, r, :], acc[:, u, :], RELU, bias=bias[:, r : r + 1])
+            nc.sync.dma_start(y_rows[:, :, cols], y[:])
+            y_bf = sb.tile([P, CHUNK * PACK], BF16, name=f"y_bf{c}", align_bytes=64)
+            nc.vector.tensor_copy(woven(y_bf[:]), planar(y[:]))
+            nc.vector.quantize_mx(y_codes[:, cols].bitcast(FP8X4), y_scales[:, cols], y_bf[:])
+            if c % 2 == 1:
+                pair = slice((c - 1) * CHUNK, (c + 1) * CHUNK)
+                nc.sync.dma_start(y_words[:, pair], y_codes[:, pair])
+        for quad in range(4):
+            queue = nc.sync if quad % 2 == 0 else nc.scalar
+            queue.dma_start(
+                out_2[0, 4 * quad : 4 * quad + 4, :].bitcast(I32),
+                y_scales[32 * quad : 32 * quad + 4, :].bitcast(I32),
+            )

@@ -29,11 +29,11 @@ BYTES = D * NQ * 4 + P * T * 4 + 16 * T + T * 4 + P * 32 * 2 + N * NQ * 4 + N * 
 
 
 def woven(tile):
-    return tile.rearrange("p (c i t) -> p c t i", i=4, t=PACK)
+    return tile.rearrange("p (c t) -> p c t", t=PACK)
 
 
 def planar(rows):
-    return rows.rearrange("p t (c i) -> p c t i", i=4)
+    return rows.rearrange("p t c -> p c t")
 
 
 def tile_attend_plh_brelu_topk_kernel(tc, qT, k_words, k_scales, nb, offs, out_0, out_1, out_2):
@@ -45,41 +45,41 @@ def tile_attend_plh_brelu_topk_kernel(tc, qT, k_words, k_scales, nb, offs, out_0
         offsets = sb.tile([P, N // 16], U16, name="offsets")
         nc.sync.dma_start(offsets[:], offs)
 
-        ks = sb.tile([P, T], U8, name="ks", tag="scales_then_words", align_bytes=64)
+        ks = sb.tile([P, T], U8, name="ks", align_bytes=64)
         nc.vector.memset(ks[:].bitcast(I32), 0)
         for quad in range(4):
-            nc.scalar.dma_start(
+            nc.sync.dma_start(
                 ks[32 * quad : 32 * quad + 4, :].bitcast(I32),
                 k_scales[0, 4 * quad : 4 * quad + 4, :].bitcast(I32),
             )
-        nbt = sb.tile([P, T], F32, name="nbt", tag="bias_then_queries")
+        nbt = sb.tile([P, T], F32, name="nbt")
         nc.sync.dma_start(nbt[BIAS_ROW:P, :], nb[0:1, :])
         nc.vector.memset(nbt[0:BIAS_ROW, :], 0.0)
 
-        kw = sb.tile([P, T], I32, name="kw", tag="words_then_codes", align_bytes=64)
+        kw = sb.tile([P, T], I32, name="kw", align_bytes=64)
         nc.sync.dma_start(kw[:], k_words[0].rearrange("p t r -> p (t r)").bitcast(I32))
 
         q_rows = qT[0].rearrange("(p j) q -> p j q", j=PACK)
-        q_raw0 = sb.tile([P, PACK, LOAD], F32, name="q_raw0")
+        q_raw0 = sb.tile([P, PACK, LOAD], F32, name="q_raw0", tag="queries_then_bias")
         nc.sync.dma_start(q_raw0[:], q_rows[:, :, 0:LOAD])
 
         ident = sb.tile([P, P], F32, name="ident")
         make_identity(nc, ident[:])
 
-        nbg = sb.tile([P, N], F32, name="nbg")
-        nc.vector.tensor_copy(nbg[:], nbt[:].indirect(offsets[:]))
-        q_raw1 = sb.tile([P, PACK, LOAD], F32, name="q_raw1", tag="bias_then_queries")
+        q_raw1 = sb.tile([P, PACK, LOAD], F32, name="q_raw1")
         nc.sync.dma_start(q_raw1[:], q_rows[:, :, LOAD : 2 * LOAD])
         q_raw = [q_raw0, q_raw1]
 
         ksg = sb.tile([P, N], U8, name="ksg", align_bytes=64)
         nc.vector.tensor_copy(ksg[:], ks[:].indirect(offsets[:]))
+        nbg = sb.tile([P, N], F32, name="nbg")
+        nc.vector.tensor_copy(nbg[:], nbt[:].indirect(offsets[:]))
         ksd = sb.tile([P, N], U8, name="ksd", align_bytes=64)
         nc.vector.tensor_copy(
-            ksd[:].rearrange("p (r s) -> p s r", r=PACK),
-            ksg[:].rearrange("p (s r) -> p s r", r=PACK),
+            ksd[:].rearrange("p (r c i) -> p c r i", r=PACK, i=16),
+            ksg[:].rearrange("p (c i r) -> p c r i", r=PACK, i=16),
         )
-        kg = sb.tile([P, N], U32, name="kg", tag="scales_then_words", align_bytes=64)
+        kg = sb.tile([P, N], U32, name="kg", align_bytes=64)
         nc.vector.tensor_copy(
             kg[:].rearrange("p (r s) -> p s r", r=PACK),
             kw[:].bitcast(U32).indirect(offsets[:]),
@@ -88,15 +88,12 @@ def tile_attend_plh_brelu_topk_kernel(tc, qT, k_words, k_scales, nb, offs, out_0
         bias_ps = ps.tile([P, PACK, P], F32, name="bias_ps", tag="bank7")
         for r in range(PACK):
             nc.tensor.transpose(bias_ps[:, r, :], nbg[:, r::PACK], ident[:])
-        bias = sb.tile([P, PACK], F32, name="bias")
-        nc.scalar.copy(bias[:], bias_ps[:, :, BIAS_ROW])
 
         y_codes = sb.tile([P, NQ], I32, name="y_codes", align_bytes=64)
         y_scales = sb.tile([P, NQ], U8, name="y_scales", align_bytes=64)
         y_rows = out_0.rearrange("(p r) q -> p r q", r=PACK)
         y_words = out_1[0].rearrange("p q u -> p (q u)").bitcast(I32)
-        q_codes = sb.tile([P, NQ], U32, name="q_codes", tag="words_then_codes", align_bytes=64)
-        q_scales = sb.tile([P, NQ], U8, name="q_scales", align_bytes=64)
+        q_codes, q_scales = [], []
 
         n_chunks = NQ // CHUNK
         last = n_chunks - 1
@@ -109,7 +106,14 @@ def tile_attend_plh_brelu_topk_kernel(tc, qT, k_words, k_scales, nb, offs, out_0
                 nc.vector.tensor_copy(woven(q_bf[:]), src)
             else:
                 nc.scalar.copy(woven(q_bf[:]), src)
-            nc.vector.quantize_mx(q_codes[:, cols].bitcast(FP8X4), q_scales[:, cols], q_bf[:])
+            codes = sb.tile([P, CHUNK], U32, name=f"q_codes{c}", align_bytes=64)
+            scales = sb.tile([P, CHUNK], U8, name=f"q_scales{c}", align_bytes=64)
+            nc.vector.quantize_mx(codes[:].bitcast(FP8X4), scales[:], q_bf[:])
+            q_codes.append(codes)
+            q_scales.append(scales)
+            if c == 1:
+                bias = sb.tile([P, PACK], F32, name="bias", tag="queries_then_bias")
+                nc.scalar.copy(bias[:], bias_ps[:, :, BIAS_ROW])
 
         for c in range(n_chunks):
             cols = slice(c * CHUNK, (c + 1) * CHUNK)
@@ -122,8 +126,8 @@ def tile_attend_plh_brelu_topk_kernel(tc, qT, k_words, k_scales, nb, offs, out_0
                         acc[:, u, :],
                         lhsT=kg[:, r * P : (r + 1) * P].bitcast(FP8X4),
                         lhsT_scale=ksd[:, r * P : (r + 1) * P],
-                        rhs=q_codes[:, cols].bitcast(FP8X4),
-                        rhs_scale=q_scales[:, cols],
+                        rhs=q_codes[c][:].bitcast(FP8X4),
+                        rhs_scale=q_scales[c][:],
                         start=True,
                         stop=True,
                     )

@@ -18,7 +18,6 @@ T = 2048
 N = 512
 NQ = 512
 D = 512
-LOAD = 256
 CHUNK = 128
 BIAS_ROW = P - 1
 ADD = mybir.AluOpType.add
@@ -44,82 +43,80 @@ def tile_attend_plh_brelu_topk_kernel(tc, qT, k_words, k_scales, nb, offs, out_0
 
         offsets = sb.tile([P, N // 16], U16, name="offsets")
         nc.sync.dma_start(offsets[:], offs)
+        nbt = sb.tile([P, T], F32, name="nbt")
+        nc.sync.dma_start(nbt[BIAS_ROW:P, :], nb[0:1, :])
 
-        ks = sb.tile([P, T], U8, name="ks", align_bytes=64)
+        q_rows = qT[0].rearrange("(p j) q -> p j q", j=PACK)
+        q_head = sb.tile([P, PACK, CHUNK], F32, name="q_head", tag="queries_then_scales", align_bytes=64)
+        nc.sync.dma_start(q_head[:], q_rows[:, :, 0:CHUNK])
+
+        ks = sb.tile([P, T], U8, name="ks")
         nc.vector.memset(ks[:].bitcast(I32), 0)
         for quad in range(4):
             nc.sync.dma_start(
                 ks[32 * quad : 32 * quad + 4, :].bitcast(I32),
                 k_scales[0, 4 * quad : 4 * quad + 4, :].bitcast(I32),
             )
-        nbt = sb.tile([P, T], F32, name="nbt")
-        nc.sync.dma_start(nbt[BIAS_ROW:P, :], nb[0:1, :])
         nc.vector.memset(nbt[0:BIAS_ROW, :], 0.0)
 
-        kw = sb.tile([P, T], I32, name="kw", align_bytes=64)
+        kw = sb.tile([P, T], I32, name="kw")
         nc.sync.dma_start(kw[:], k_words[0].rearrange("p t r -> p (t r)").bitcast(I32))
-
-        q_rows = qT[0].rearrange("(p j) q -> p j q", j=PACK)
-        q_raw0 = sb.tile([P, PACK, LOAD], F32, name="q_raw0", tag="queries_then_bias")
-        nc.sync.dma_start(q_raw0[:], q_rows[:, :, 0:LOAD])
+        q_mid = sb.tile([P, PACK, 2 * CHUNK], F32, name="q_mid", tag="queries_then_result")
+        nc.sync.dma_start(q_mid[:], q_rows[:, :, CHUNK : 3 * CHUNK])
+        q_tail = sb.tile([P, PACK, CHUNK], F32, name="q_tail")
+        nc.sync.dma_start(q_tail[:], q_rows[:, :, 3 * CHUNK : 4 * CHUNK])
+        q_raw = [q_head[:], q_mid[:, :, 0:CHUNK], q_mid[:, :, CHUNK : 2 * CHUNK], q_tail[:]]
 
         ident = sb.tile([P, P], F32, name="ident")
         make_identity(nc, ident[:])
 
-        q_raw1 = sb.tile([P, PACK, LOAD], F32, name="q_raw1")
-        nc.sync.dma_start(q_raw1[:], q_rows[:, :, LOAD : 2 * LOAD])
-        q_raw = [q_raw0, q_raw1]
-
-        ksg = sb.tile([P, N], U8, name="ksg", align_bytes=64)
-        nc.vector.tensor_copy(ksg[:], ks[:].indirect(offsets[:]))
         nbg = sb.tile([P, N], F32, name="nbg")
         nc.vector.tensor_copy(nbg[:], nbt[:].indirect(offsets[:]))
-        ksd = sb.tile([P, N], U8, name="ksd", align_bytes=64)
-        nc.vector.tensor_copy(
-            ksd[:].rearrange("p (r c i) -> p c r i", r=PACK, i=16),
-            ksg[:].rearrange("p (c i r) -> p c r i", r=PACK, i=16),
-        )
-        kg = sb.tile([P, N], U32, name="kg", align_bytes=64)
-        nc.vector.tensor_copy(
-            kg[:].rearrange("p (r s) -> p s r", r=PACK),
-            kw[:].bitcast(U32).indirect(offsets[:]),
-        )
-
+        ksg = sb.tile([P, N], U8, name="ksg")
+        nc.vector.tensor_copy(ksg[:], ks[:].indirect(offsets[:]))
         bias_ps = ps.tile([P, PACK, P], F32, name="bias_ps", tag="bank7")
         for r in range(PACK):
             nc.tensor.transpose(bias_ps[:, r, :], nbg[:, r::PACK], ident[:])
+        bias = sb.tile([P, PACK], F32, name="bias")
+        nc.scalar.copy(bias[:], bias_ps[:, :, BIAS_ROW])
 
         y_codes = sb.tile([P, NQ], I32, name="y_codes", align_bytes=64)
         y_scales = sb.tile([P, NQ], U8, name="y_scales", align_bytes=64)
         y_rows = out_0.rearrange("(p r) q -> p r q", r=PACK)
         y_words = out_1[0].rearrange("p q u -> p (q u)").bitcast(I32)
-        q_codes, q_scales = [], []
 
         n_chunks = NQ // CHUNK
         last = n_chunks - 1
+        q_codes, q_scales = [], []
         for c in range(n_chunks):
-            cols = slice(c * CHUNK, (c + 1) * CHUNK)
-            at = (c * CHUNK) % LOAD
-            src = planar(q_raw[c * CHUNK // LOAD][:, :, at : at + CHUNK])
             q_bf = sb.tile([P, CHUNK * PACK], BF16, name=f"q_bf{c}", align_bytes=64)
             if c == last:
-                nc.vector.tensor_copy(woven(q_bf[:]), src)
+                nc.vector.tensor_copy(woven(q_bf[:]), planar(q_raw[c]))
             else:
-                nc.scalar.copy(woven(q_bf[:]), src)
+                nc.scalar.copy(woven(q_bf[:]), planar(q_raw[c]))
             codes = sb.tile([P, CHUNK], U32, name=f"q_codes{c}", align_bytes=64)
             scales = sb.tile([P, CHUNK], U8, name=f"q_scales{c}", align_bytes=64)
             nc.vector.quantize_mx(codes[:].bitcast(FP8X4), scales[:], q_bf[:])
             q_codes.append(codes)
             q_scales.append(scales)
-            if c == 1:
-                bias = sb.tile([P, PACK], F32, name="bias", tag="queries_then_bias")
-                nc.scalar.copy(bias[:], bias_ps[:, :, BIAS_ROW])
+            if c == 0:
+                ksd = sb.tile([P, N], U8, name="ksd", tag="queries_then_scales", align_bytes=64)
+                nc.vector.tensor_copy(
+                    ksd[:].rearrange("p (r c i) -> p c r i", r=PACK, i=16),
+                    ksg[:].rearrange("p (c i r) -> p c r i", r=PACK, i=16),
+                )
+                kg = sb.tile([P, N], U32, name="kg", align_bytes=64)
+                nc.vector.tensor_copy(
+                    kg[:].rearrange("p (r s) -> p s r", r=PACK),
+                    kw[:].bitcast(U32).indirect(offsets[:]),
+                )
 
         for c in range(n_chunks):
             cols = slice(c * CHUNK, (c + 1) * CHUNK)
-            y = sb.tile([P, PACK, CHUNK], F32, name=f"y{c}")
+            y = sb.tile([P, PACK, CHUNK], F32, name=f"y{c}", tag="queries_then_result" if c == 0 else f"y{c}")
             for h in range(2):
-                acc = ps.tile([P, 2, CHUNK], F32, name=f"acc{c}_{h}", tag=f"bank{2 * c + h}")
+                bank = 2 * c + h
+                acc = ps.tile([P, 2, CHUNK], F32, name=f"acc{bank}", tag=f"bank{bank}")
                 for u in range(2):
                     r = 2 * h + u
                     nc.tensor.matmul_mx(
@@ -133,13 +130,18 @@ def tile_attend_plh_brelu_topk_kernel(tc, qT, k_words, k_scales, nb, offs, out_0
                     )
                 for u in range(2):
                     r = 2 * h + u
-                    if c == last and h == 1:
+                    if bank in (2,):
                         nc.vector.tensor_scalar(y[:, r, :], acc[:, u, :], bias[:, r : r + 1], 0.0, ADD, MAX)
                     else:
                         nc.scalar.activation(y[:, r, :], acc[:, u, :], RELU, bias=bias[:, r : r + 1])
             nc.sync.dma_start(y_rows[:, :, cols], y[:])
             y_bf = sb.tile([P, CHUNK * PACK], BF16, name=f"y_bf{c}", align_bytes=64)
-            nc.vector.tensor_copy(woven(y_bf[:]), planar(y[:]))
+            if c == last:
+                half = CHUNK // 2
+                nc.scalar.copy(woven(y_bf[:, 0 : half * PACK]), planar(y[:, :, 0:half]))
+                nc.vector.tensor_copy(woven(y_bf[:, half * PACK :]), planar(y[:, :, half:]))
+            else:
+                nc.vector.tensor_copy(woven(y_bf[:]), planar(y[:]))
             nc.vector.quantize_mx(y_codes[:, cols].bitcast(FP8X4), y_scales[:, cols], y_bf[:])
             if c % 2 == 1:
                 pair = slice((c - 1) * CHUNK, (c + 1) * CHUNK)

@@ -89,8 +89,8 @@ def tile_attend_plh_brelu_topk_kernel(tc, qT, k_words, k_scales, nb, offs, out_0
         last = n_chunks - 1
         q_codes, q_scales = [], []
         for c in range(n_chunks):
-            q_bf = sb.tile([P, CHUNK * PACK], BF16, name=f"q_bf{c}", align_bytes=64)
-            if c == last:
+            q_bf = sb.tile([P, CHUNK * PACK], BF16, name=f"q_bf{c}", tag="q_bf_odd" if c % 2 == 1 else f"q_bf{c}", align_bytes=64)
+            if c % 2 == 1:
                 nc.vector.tensor_copy(woven(q_bf[:]), planar(q_raw[c]))
             else:
                 nc.scalar.copy(woven(q_bf[:]), planar(q_raw[c]))
@@ -130,7 +130,7 @@ def tile_attend_plh_brelu_topk_kernel(tc, qT, k_words, k_scales, nb, offs, out_0
                     )
                 for u in range(2):
                     r = 2 * h + u
-                    if bank in (2,):
+                    if bank in (5,):
                         nc.vector.tensor_scalar(y[:, r, :], acc[:, u, :], bias[:, r : r + 1], 0.0, ADD, MAX)
                     else:
                         nc.scalar.activation(y[:, r, :], acc[:, u, :], RELU, bias=bias[:, r : r + 1])

@@ -28,11 +28,11 @@ BYTES = D * NQ * 4 + P * T * 4 + 16 * T + T * 4 + P * 32 * 2 + N * NQ * 4 + N * 
 
 
 def woven(tile):
-    return tile.rearrange("p (c t) -> p c t", t=PACK)
+    return tile.rearrange("p (c i t) -> p c t i", t=PACK, i=4)
 
 
 def planar(rows):
-    return rows.rearrange("p t c -> p c t")
+    return rows.rearrange("p t (c i) -> p c t i", i=4)
 
 
 def tile_attend_plh_brelu_topk_kernel(tc, qT, k_words, k_scales, nb, offs, out_0, out_1, out_2):
@@ -40,6 +40,8 @@ def tile_attend_plh_brelu_topk_kernel(tc, qT, k_words, k_scales, nb, offs, out_0
     with ExitStack() as ctx:
         sb = ctx.enter_context(tc.tile_pool(name="sb", bufs=1))
         ps = ctx.enter_context(tc.psum_pool(name="ps", bufs=1))
+        n_chunks = NQ // CHUNK
+        last = n_chunks - 1
 
         offsets = sb.tile([P, N // 16], U16, name="offsets")
         nc.sync.dma_start(offsets[:], offs)
@@ -47,28 +49,24 @@ def tile_attend_plh_brelu_topk_kernel(tc, qT, k_words, k_scales, nb, offs, out_0
         nc.sync.dma_start(nbt[BIAS_ROW:P, :], nb[0:1, :])
 
         q_rows = qT[0].rearrange("(p j) q -> p j q", j=PACK)
-        q_head = sb.tile([P, PACK, CHUNK], F32, name="q_head", tag="queries_then_scales", align_bytes=64)
-        nc.sync.dma_start(q_head[:], q_rows[:, :, 0:CHUNK])
+        q_tags = ["queries_then_scales", "queries_then_result", "q_raw2", "q_raw3"]
+        q_raw = [sb.tile([P, PACK, CHUNK], F32, name=f"q_raw{c}", tag=q_tags[c], align_bytes=64) for c in range(n_chunks)]
+        nc.sync.dma_start(q_raw[0][:], q_rows[:, :, 0:CHUNK])
 
         ks = sb.tile([P, T], U8, name="ks")
         nc.vector.memset(ks[:].bitcast(I32), 0)
-        for quad in range(4):
-            nc.sync.dma_start(
-                ks[32 * quad : 32 * quad + 4, :].bitcast(I32),
-                k_scales[0, 4 * quad : 4 * quad + 4, :].bitcast(I32),
-            )
+        for j in range(4):
+            nc.sync.dma_start(ks[j:P:32, :].bitcast(I32), k_scales[0, j:16:4, :].bitcast(I32))
         nc.vector.memset(nbt[0:BIAS_ROW, :], 0.0)
 
         kw = sb.tile([P, T], I32, name="kw")
         nc.sync.dma_start(kw[:], k_words[0].rearrange("p t r -> p (t r)").bitcast(I32))
-        q_mid = sb.tile([P, PACK, 2 * CHUNK], F32, name="q_mid", tag="queries_then_result")
-        nc.sync.dma_start(q_mid[:], q_rows[:, :, CHUNK : 3 * CHUNK])
-        q_tail = sb.tile([P, PACK, CHUNK], F32, name="q_tail")
-        nc.sync.dma_start(q_tail[:], q_rows[:, :, 3 * CHUNK : 4 * CHUNK])
-        q_raw = [q_head[:], q_mid[:, :, 0:CHUNK], q_mid[:, :, CHUNK : 2 * CHUNK], q_tail[:]]
+        for c in range(1, n_chunks):
+            nc.sync.dma_start(q_raw[c][:], q_rows[:, :, c * CHUNK : (c + 1) * CHUNK])
 
         ident = sb.tile([P, P], F32, name="ident")
-        make_identity(nc, ident[:])
+        nc.vector.memset(ident[:], 0.0)
+        make_identity(nc, ident[:], nomemset=True)
 
         nbg = sb.tile([P, N], F32, name="nbg")
         nc.vector.tensor_copy(nbg[:], nbt[:].indirect(offsets[:]))
@@ -85,15 +83,13 @@ def tile_attend_plh_brelu_topk_kernel(tc, qT, k_words, k_scales, nb, offs, out_0
         y_rows = out_0.rearrange("(p r) q -> p r q", r=PACK)
         y_words = out_1[0].rearrange("p q u -> p (q u)").bitcast(I32)
 
-        n_chunks = NQ // CHUNK
-        last = n_chunks - 1
         q_codes, q_scales = [], []
         for c in range(n_chunks):
-            q_bf = sb.tile([P, CHUNK * PACK], BF16, name=f"q_bf{c}", tag="q_bf_odd" if c % 2 == 1 else f"q_bf{c}", align_bytes=64)
-            if c % 2 == 1:
-                nc.vector.tensor_copy(woven(q_bf[:]), planar(q_raw[c]))
+            q_bf = sb.tile([P, CHUNK * PACK], BF16, name=f"q_bf{c}", tag=f"bf{c}", align_bytes=64)
+            if c < 2:
+                nc.scalar.copy(woven(q_bf[:]), planar(q_raw[c][:]))
             else:
-                nc.scalar.copy(woven(q_bf[:]), planar(q_raw[c]))
+                nc.vector.tensor_copy(woven(q_bf[:]), planar(q_raw[c][:]))
             codes = sb.tile([P, CHUNK], U32, name=f"q_codes{c}", align_bytes=64)
             scales = sb.tile([P, CHUNK], U8, name=f"q_scales{c}", align_bytes=64)
             nc.vector.quantize_mx(codes[:].bitcast(FP8X4), scales[:], q_bf[:])
@@ -111,9 +107,10 @@ def tile_attend_plh_brelu_topk_kernel(tc, qT, k_words, k_scales, nb, offs, out_0
                     kw[:].bitcast(U32).indirect(offsets[:]),
                 )
 
+        y_pair = [sb.tile([P, 2 * CHUNK * PACK], BF16, name=f"y_bf{u}", align_bytes=64) for u in range(2)]
         for c in range(n_chunks):
             cols = slice(c * CHUNK, (c + 1) * CHUNK)
-            y = sb.tile([P, PACK, CHUNK], F32, name=f"y{c}", tag="queries_then_result" if c == 0 else f"y{c}")
+            y = sb.tile([P, PACK, CHUNK], F32, name=f"y{c}", tag="queries_then_result" if c == 0 else f"y{c}", align_bytes=64)
             for h in range(2):
                 bank = 2 * c + h
                 acc = ps.tile([P, 2, CHUNK], F32, name=f"acc{bank}", tag=f"bank{bank}")
@@ -130,25 +127,19 @@ def tile_attend_plh_brelu_topk_kernel(tc, qT, k_words, k_scales, nb, offs, out_0
                     )
                 for u in range(2):
                     r = 2 * h + u
-                    if bank in (5,):
-                        nc.vector.tensor_scalar(y[:, r, :], acc[:, u, :], bias[:, r : r + 1], 0.0, ADD, MAX)
-                    else:
-                        nc.scalar.activation(y[:, r, :], acc[:, u, :], RELU, bias=bias[:, r : r + 1])
+                    nc.scalar.activation(y[:, r, :], acc[:, u, :], RELU, bias=bias[:, r : r + 1])
             nc.sync.dma_start(y_rows[:, :, cols], y[:])
-            y_bf = sb.tile([P, CHUNK * PACK], BF16, name=f"y_bf{c}", align_bytes=64)
+            y_bf = y_pair[c // 2][:, (c % 2) * CHUNK * PACK : (c % 2 + 1) * CHUNK * PACK]
             if c == last:
                 half = CHUNK // 2
                 nc.scalar.copy(woven(y_bf[:, 0 : half * PACK]), planar(y[:, :, 0:half]))
                 nc.vector.tensor_copy(woven(y_bf[:, half * PACK :]), planar(y[:, :, half:]))
             else:
-                nc.vector.tensor_copy(woven(y_bf[:]), planar(y[:]))
-            nc.vector.quantize_mx(y_codes[:, cols].bitcast(FP8X4), y_scales[:, cols], y_bf[:])
+                nc.vector.tensor_copy(woven(y_bf), planar(y[:]))
             if c % 2 == 1:
                 pair = slice((c - 1) * CHUNK, (c + 1) * CHUNK)
+                nc.vector.quantize_mx(y_codes[:, pair].bitcast(FP8X4), y_scales[:, pair], y_pair[c // 2][:])
                 nc.sync.dma_start(y_words[:, pair], y_codes[:, pair])
-        for quad in range(4):
-            queue = nc.sync if quad % 2 == 0 else nc.scalar
-            queue.dma_start(
-                out_2[0, 4 * quad : 4 * quad + 4, :].bitcast(I32),
-                y_scales[32 * quad : 32 * quad + 4, :].bitcast(I32),
-            )
+        for j in range(4):
+            queue = nc.sync if j % 2 == 0 else nc.scalar
+            queue.dma_start(out_2[0, j:16:4, :].bitcast(I32), y_scales[j:P:32, :].bitcast(I32))

@@ -39,6 +39,7 @@ def tile_attend_plh_brelu_topk_kernel(tc, qT, k_words, k_scales, nb, offs, out_0
     nc = tc.nc
     with ExitStack() as ctx:
         sb = ctx.enter_context(tc.tile_pool(name="sb", bufs=1))
+        held = ctx.enter_context(tc.tile_pool(name="held", bufs=1))
         ps = ctx.enter_context(tc.psum_pool(name="ps", bufs=1))
         n_chunks = NQ // CHUNK
         last = n_chunks - 1
@@ -46,11 +47,15 @@ def tile_attend_plh_brelu_topk_kernel(tc, qT, k_words, k_scales, nb, offs, out_0
         offsets = sb.tile([P, N // 16], U16, name="offsets")
         nc.sync.dma_start(offsets[:], offs)
         nbt = sb.tile([P, T], F32, name="nbt")
-        nc.sync.dma_start(nbt[BIAS_ROW:P, :], nb[0:1, :])
+        nc.scalar.dma_start(nbt[BIAS_ROW:P, :], nb[0:1, :])
 
         q_rows = qT[0].rearrange("(p j) q -> p j q", j=PACK)
-        q_tags = ["queries_then_scales", "queries_then_result", "q_raw2", "q_raw3"]
-        q_raw = [sb.tile([P, PACK, CHUNK], F32, name=f"q_raw{c}", tag=q_tags[c], align_bytes=64) for c in range(n_chunks)]
+        q_raw = [
+            sb.tile([P, PACK, CHUNK], F32, name="q_raw0", tag="queries_then_scales", align_bytes=64),
+            held.tile([P, PACK, CHUNK], F32, name="q_raw1", offset=0, align_bytes=64),
+            sb.tile([P, PACK, CHUNK], F32, name="q_raw2"),
+            sb.tile([P, PACK, CHUNK], F32, name="q_raw3", tag="queries_then_rounded", align_bytes=64),
+        ]
         nc.sync.dma_start(q_raw[0][:], q_rows[:, :, 0:CHUNK])
 
         ks = sb.tile([P, T], U8, name="ks")
@@ -85,7 +90,10 @@ def tile_attend_plh_brelu_topk_kernel(tc, qT, k_words, k_scales, nb, offs, out_0
 
         q_codes, q_scales = [], []
         for c in range(n_chunks):
-            q_bf = sb.tile([P, CHUNK * PACK], BF16, name=f"q_bf{c}", tag=f"bf{c}", align_bytes=64)
+            if c == 2:
+                q_bf = held.tile([P, CHUNK * PACK], BF16, name="q_bf2", offset=0, align_bytes=64)
+            else:
+                q_bf = sb.tile([P, CHUNK * PACK], BF16, name=f"q_bf{c}", align_bytes=64)
             if c < 2:
                 nc.scalar.copy(woven(q_bf[:]), planar(q_raw[c][:]))
             else:
@@ -107,10 +115,16 @@ def tile_attend_plh_brelu_topk_kernel(tc, qT, k_words, k_scales, nb, offs, out_0
                     kw[:].bitcast(U32).indirect(offsets[:]),
                 )
 
-        y_pair = [sb.tile([P, 2 * CHUNK * PACK], BF16, name=f"y_bf{u}", align_bytes=64) for u in range(2)]
+        y_pair = [
+            sb.tile([P, 2 * CHUNK * PACK], BF16, name="y_bf0", tag="queries_then_rounded", align_bytes=64),
+            sb.tile([P, 2 * CHUNK * PACK], BF16, name="y_bf1", align_bytes=64),
+        ]
         for c in range(n_chunks):
             cols = slice(c * CHUNK, (c + 1) * CHUNK)
-            y = sb.tile([P, PACK, CHUNK], F32, name=f"y{c}", tag="queries_then_result" if c == 0 else f"y{c}", align_bytes=64)
+            if c == 0:
+                y = held.tile([P, PACK, CHUNK], F32, name="y0", offset=1024, align_bytes=64)
+            else:
+                y = sb.tile([P, PACK, CHUNK], F32, name=f"y{c}")
             for h in range(2):
                 bank = 2 * c + h
                 acc = ps.tile([P, 2, CHUNK], F32, name=f"acc{bank}", tag=f"bank{bank}")
@@ -136,9 +150,12 @@ def tile_attend_plh_brelu_topk_kernel(tc, qT, k_words, k_scales, nb, offs, out_0
                 nc.vector.tensor_copy(woven(y_bf[:, half * PACK :]), planar(y[:, :, half:]))
             else:
                 nc.vector.tensor_copy(woven(y_bf), planar(y[:]))
+            if c >= 2:
+                nc.vector.quantize_mx(y_codes[:, cols].bitcast(FP8X4), y_scales[:, cols], y_bf)
             if c % 2 == 1:
                 pair = slice((c - 1) * CHUNK, (c + 1) * CHUNK)
-                nc.vector.quantize_mx(y_codes[:, pair].bitcast(FP8X4), y_scales[:, pair], y_pair[c // 2][:])
+                if c == 1:
+                    nc.vector.quantize_mx(y_codes[:, pair].bitcast(FP8X4), y_scales[:, pair], y_pair[0][:])
                 nc.sync.dma_start(y_words[:, pair], y_codes[:, pair])
         for j in range(4):
             queue = nc.sync if j % 2 == 0 else nc.scalar

@@ -44,87 +44,87 @@ def tile_attend_plh_brelu_topk_kernel(tc, qT, k_words, k_scales, nb, offs, out_0
         n_chunks = NQ // CHUNK
         last = n_chunks - 1
 
-        offsets = sb.tile([P, N // 16], U16, name="offsets")
+        offsets = sb.tile([P, N // 16], U16, name="offsets", align_bytes=256)
         nc.sync.dma_start(offsets[:], offs)
-        nbt = sb.tile([P, T], F32, name="nbt")
+        nbt = sb.tile([P, T], F32, name="nbt", align_bytes=256)
         nc.scalar.dma_start(nbt[BIAS_ROW:P, :], nb[0:1, :])
 
         q_rows = qT[0].rearrange("(p j) q -> p j q", j=PACK)
         q_raw = [
-            sb.tile([P, PACK, CHUNK], F32, name="q_raw0", tag="queries_then_scales", align_bytes=64),
-            held.tile([P, PACK, CHUNK], F32, name="q_raw1", offset=0, align_bytes=64),
-            sb.tile([P, PACK, CHUNK], F32, name="q_raw2"),
-            sb.tile([P, PACK, CHUNK], F32, name="q_raw3", tag="queries_then_rounded", align_bytes=64),
+            sb.tile([P, PACK, CHUNK], F32, name="q_raw0", tag="queries_then_scales", align_bytes=256),
+            held.tile([P, PACK, CHUNK], F32, name="q_raw1", offset=0, align_bytes=256),
+            sb.tile([P, PACK, CHUNK], F32, name="q_raw2", align_bytes=256),
+            sb.tile([P, PACK, CHUNK], F32, name="q_raw3", tag="queries_then_rounded", align_bytes=256),
         ]
         nc.sync.dma_start(q_raw[0][:], q_rows[:, :, 0:CHUNK])
 
-        ks = sb.tile([P, T], U8, name="ks")
+        ks = sb.tile([P, T], U8, name="ks", align_bytes=256)
         nc.vector.memset(ks[:].bitcast(I32), 0)
         for j in range(4):
             nc.sync.dma_start(ks[j:P:32, :].bitcast(I32), k_scales[0, j:16:4, :].bitcast(I32))
         nc.vector.memset(nbt[0:BIAS_ROW, :], 0.0)
 
-        kw = sb.tile([P, T], I32, name="kw")
+        kw = sb.tile([P, T], I32, name="kw", align_bytes=256)
         nc.sync.dma_start(kw[:], k_words[0].rearrange("p t r -> p (t r)").bitcast(I32))
         for c in range(1, n_chunks):
             nc.sync.dma_start(q_raw[c][:], q_rows[:, :, c * CHUNK : (c + 1) * CHUNK])
 
-        ident = sb.tile([P, P], F32, name="ident")
+        ident = sb.tile([P, P], F32, name="ident", align_bytes=256)
         nc.vector.memset(ident[:], 0.0)
         make_identity(nc, ident[:], nomemset=True)
 
-        nbg = sb.tile([P, N], F32, name="nbg")
+        nbg = sb.tile([P, N], F32, name="nbg", align_bytes=256)
         nc.vector.tensor_copy(nbg[:], nbt[:].indirect(offsets[:]))
-        ksg = sb.tile([P, N], U8, name="ksg")
+        ksg = sb.tile([P, N], U8, name="ksg", align_bytes=256)
         nc.vector.tensor_copy(ksg[:], ks[:].indirect(offsets[:]))
         bias_ps = ps.tile([P, PACK, P], F32, name="bias_ps", tag="bank7")
         for r in range(PACK):
             nc.tensor.transpose(bias_ps[:, r, :], nbg[:, r::PACK], ident[:])
-        bias = sb.tile([P, PACK], F32, name="bias")
+        bias = sb.tile([P, PACK], F32, name="bias", align_bytes=256)
         nc.scalar.copy(bias[:], bias_ps[:, :, BIAS_ROW])
 
-        y_codes = sb.tile([P, NQ], I32, name="y_codes", align_bytes=64)
-        y_scales = sb.tile([P, NQ], U8, name="y_scales", align_bytes=64)
+        y_codes = sb.tile([P, NQ], I32, name="y_codes", align_bytes=256)
+        y_scales = sb.tile([P, NQ], U8, name="y_scales", align_bytes=256)
         y_rows = out_0.rearrange("(p r) q -> p r q", r=PACK)
         y_words = out_1[0].rearrange("p q u -> p (q u)").bitcast(I32)
 
         q_codes, q_scales = [], []
         for c in range(n_chunks):
             if c == 2:
-                q_bf = held.tile([P, CHUNK * PACK], BF16, name="q_bf2", offset=0, align_bytes=64)
+                q_bf = held.tile([P, CHUNK * PACK], BF16, name="q_bf2", offset=0, align_bytes=256)
             else:
-                q_bf = sb.tile([P, CHUNK * PACK], BF16, name=f"q_bf{c}", align_bytes=64)
+                q_bf = sb.tile([P, CHUNK * PACK], BF16, name=f"q_bf{c}", align_bytes=256)
             if c < 2:
                 nc.scalar.copy(woven(q_bf[:]), planar(q_raw[c][:]))
             else:
                 nc.vector.tensor_copy(woven(q_bf[:]), planar(q_raw[c][:]))
-            codes = sb.tile([P, CHUNK], U32, name=f"q_codes{c}", align_bytes=64)
-            scales = sb.tile([P, CHUNK], U8, name=f"q_scales{c}", align_bytes=64)
+            codes = sb.tile([P, CHUNK], U32, name=f"q_codes{c}", align_bytes=256)
+            scales = sb.tile([P, CHUNK], U8, name=f"q_scales{c}", align_bytes=256)
             nc.vector.quantize_mx(codes[:].bitcast(FP8X4), scales[:], q_bf[:])
             q_codes.append(codes)
             q_scales.append(scales)
             if c == 0:
-                ksd = sb.tile([P, N], U8, name="ksd", tag="queries_then_scales", align_bytes=64)
+                ksd = sb.tile([P, N], U8, name="ksd", tag="queries_then_scales", align_bytes=256)
                 nc.vector.tensor_copy(
                     ksd[:].rearrange("p (r c i) -> p c r i", r=PACK, i=16),
                     ksg[:].rearrange("p (c i r) -> p c r i", r=PACK, i=16),
                 )
-                kg = sb.tile([P, N], U32, name="kg", align_bytes=64)
+                kg = sb.tile([P, N], U32, name="kg", align_bytes=256)
                 nc.vector.tensor_copy(
                     kg[:].rearrange("p (r s) -> p s r", r=PACK),
                     kw[:].bitcast(U32).indirect(offsets[:]),
                 )
 
         y_pair = [
-            sb.tile([P, 2 * CHUNK * PACK], BF16, name="y_bf0", tag="queries_then_rounded", align_bytes=64),
-            sb.tile([P, 2 * CHUNK * PACK], BF16, name="y_bf1", align_bytes=64),
+            sb.tile([P, 2 * CHUNK * PACK], BF16, name="y_bf0", tag="queries_then_rounded", align_bytes=256),
+            sb.tile([P, 2 * CHUNK * PACK], BF16, name="y_bf1", align_bytes=256),
         ]
         for c in range(n_chunks):
             cols = slice(c * CHUNK, (c + 1) * CHUNK)
             if c == 0:
-                y = held.tile([P, PACK, CHUNK], F32, name="y0", offset=1024, align_bytes=64)
+                y = held.tile([P, PACK, CHUNK], F32, name="y0", offset=1024, align_bytes=256)
             else:
-                y = sb.tile([P, PACK, CHUNK], F32, name=f"y{c}")
+                y = sb.tile([P, PACK, CHUNK], F32, name=f"y{c}", align_bytes=256)
             for h in range(2):
                 bank = 2 * c + h
                 acc = ps.tile([P, 2, CHUNK], F32, name=f"acc{bank}", tag=f"bank{bank}")

@@ -54,7 +54,7 @@ def tile_attend_plh_brelu_topk_kernel(tc, qT, k_words, k_scales, nb, offs, out_0
             sb.tile([P, PACK, CHUNK], F32, name="q_raw0", tag="queries_then_scales", align_bytes=256),
             held.tile([P, PACK, CHUNK], F32, name="q_raw1", offset=0, align_bytes=256),
             sb.tile([P, PACK, CHUNK], F32, name="q_raw2", align_bytes=256),
-            sb.tile([P, PACK, CHUNK], F32, name="q_raw3", tag="queries_then_rounded", align_bytes=256),
+            held.tile([P, PACK, CHUNK], F32, name="q_raw3", offset=4096, align_bytes=256),
         ]
         nc.sync.dma_start(q_raw[0][:], q_rows[:, :, 0:CHUNK])
 
@@ -116,17 +116,22 @@ def tile_attend_plh_brelu_topk_kernel(tc, qT, k_words, k_scales, nb, offs, out_0
                 )
 
         y_pair = [
-            sb.tile([P, 2 * CHUNK * PACK], BF16, name="y_bf0", tag="queries_then_rounded", align_bytes=256),
+            held.tile([P, 2 * CHUNK * PACK], BF16, name="y_bf0", offset=5120, align_bytes=256),
             sb.tile([P, 2 * CHUNK * PACK], BF16, name="y_bf1", align_bytes=256),
         ]
-        for c in range(n_chunks):
-            cols = slice(c * CHUNK, (c + 1) * CHUNK)
-            if c == 0:
-                y = held.tile([P, PACK, CHUNK], F32, name="y0", offset=1024, align_bytes=256)
-            else:
-                y = sb.tile([P, PACK, CHUNK], F32, name=f"y{c}", align_bytes=256)
-            for h in range(2):
-                bank = 2 * c + h
+        y = [
+            held.tile([P, PACK, CHUNK], F32, name="y0", offset=1024, align_bytes=256),
+            held.tile([P, PACK, CHUNK], F32, name="y1", offset=3072, align_bytes=256),
+            sb.tile([P, PACK, CHUNK], F32, name="y2", align_bytes=256),
+            sb.tile([P, PACK, CHUNK], F32, name="y3", align_bytes=256),
+        ]
+
+        def rounded(c):
+            return y_pair[c // 2][:, (c % 2) * CHUNK * PACK : (c % 2 + 1) * CHUNK * PACK]
+
+        def multiply(c):
+            for h in range(PACK // 2):
+                bank = (PACK // 2) * c + h
                 acc = ps.tile([P, 2, CHUNK], F32, name=f"acc{bank}", tag=f"bank{bank}")
                 for u in range(2):
                     r = 2 * h + u
@@ -141,22 +146,35 @@ def tile_attend_plh_brelu_topk_kernel(tc, qT, k_words, k_scales, nb, offs, out_0
                     )
                 for u in range(2):
                     r = 2 * h + u
-                    nc.scalar.activation(y[:, r, :], acc[:, u, :], RELU, bias=bias[:, r : r + 1])
-            nc.sync.dma_start(y_rows[:, :, cols], y[:])
-            y_bf = y_pair[c // 2][:, (c % 2) * CHUNK * PACK : (c % 2 + 1) * CHUNK * PACK]
-            if c == last:
-                half = CHUNK // 2
-                nc.scalar.copy(woven(y_bf[:, 0 : half * PACK]), planar(y[:, :, 0:half]))
-                nc.vector.tensor_copy(woven(y_bf[:, half * PACK :]), planar(y[:, :, half:]))
-            else:
-                nc.vector.tensor_copy(woven(y_bf), planar(y[:]))
-            if c >= 2:
-                nc.vector.quantize_mx(y_codes[:, cols].bitcast(FP8X4), y_scales[:, cols], y_bf)
+                    if c == 1 and h == 1:
+                        nc.vector.tensor_scalar(y[c][:, r, :], acc[:, u, :], bias[:, r : r + 1], 0.0, op0=ADD, op1=MAX)
+                    else:
+                        nc.scalar.activation(y[c][:, r, :], acc[:, u, :], RELU, bias=bias[:, r : r + 1])
+            nc.sync.dma_start(y_rows[:, :, c * CHUNK : (c + 1) * CHUNK], y[c][:])
+
+        def weave(c):
+            nc.vector.tensor_copy(woven(rounded(c)), planar(y[c][:]))
+
+        def quantise(c):
+            cols = slice(c * CHUNK, (c + 1) * CHUNK)
+            nc.vector.quantize_mx(y_codes[:, cols].bitcast(FP8X4), y_scales[:, cols], rounded(c))
             if c % 2 == 1:
                 pair = slice((c - 1) * CHUNK, (c + 1) * CHUNK)
-                if c == 1:
-                    nc.vector.quantize_mx(y_codes[:, pair].bitcast(FP8X4), y_scales[:, pair], y_pair[0][:])
                 nc.sync.dma_start(y_words[:, pair], y_codes[:, pair])
+
+        multiply(0)
+        multiply(1)
+        weave(0)
+        weave(1)
+        quantise(0)
+        multiply(2)
+        quantise(1)
+        weave(2)
+        multiply(3)
+        nc.vector.tensor_copy(woven(rounded(last))[:, :, 0:2, :], planar(y[last][:, 0:2, :]))
+        nc.vector.tensor_copy(woven(rounded(last))[:, :, 2:4, :], planar(y[last][:, 2:4, :]))
+        quantise(2)
+        quantise(3)
         for j in range(4):
             queue = nc.sync if j % 2 == 0 else nc.scalar
             queue.dma_start(out_2[0, j:16:4, :].bitcast(I32), y_scales[j:P:32, :].bitcast(I32))

@@ -11,6 +11,9 @@ U16 = mybir.dt.uint16
 U8 = mybir.dt.uint8
 FP8X4 = mybir.dt.float8_e4m3fn_x4
 RELU = mybir.ActivationFunctionType.Relu
+COPY = mybir.ActivationFunctionType.Copy
+ADD = mybir.AluOpType.add
+MAX = mybir.AluOpType.max
 
 P = 128
 PACK = 4
@@ -20,8 +23,8 @@ NQ = 512
 D = 512
 CHUNK = 128
 BIAS_ROW = P - 1
-ADD = mybir.AluOpType.add
-MAX = mybir.AluOpType.max
+ALIGN = 256
+SCALAR_SHARE = 32
 
 FLOPS = 2 * N * NQ * D
 BYTES = D * NQ * 4 + P * T * 4 + 16 * T + T * 4 + P * 32 * 2 + N * NQ * 4 + N * NQ + 16 * NQ
@@ -35,6 +38,10 @@ def planar(rows):
     return rows.rearrange("p t (c i) -> p c t i", i=4)
 
 
+def dealt(tile):
+    return tile.rearrange("p (r s) -> p s r", r=PACK)
+
+
 def tile_attend_plh_brelu_topk_kernel(tc, qT, k_words, k_scales, nb, offs, out_0, out_1, out_2):
     nc = tc.nc
     with ExitStack() as ctx:
@@ -44,86 +51,85 @@ def tile_attend_plh_brelu_topk_kernel(tc, qT, k_words, k_scales, nb, offs, out_0
         n_chunks = NQ // CHUNK
         last = n_chunks - 1
 
-        offsets = sb.tile([P, N // 16], U16, name="offsets", align_bytes=256)
+        offsets = sb.tile([P, N // 16], U16, name="offsets", align_bytes=ALIGN)
         nc.sync.dma_start(offsets[:], offs)
-        nbt = sb.tile([P, T], F32, name="nbt", align_bytes=256)
+        nbt = sb.tile([P, T], F32, name="nbt", align_bytes=ALIGN)
         nc.scalar.dma_start(nbt[BIAS_ROW:P, :], nb[0:1, :])
 
         q_rows = qT[0].rearrange("(p j) q -> p j q", j=PACK)
         q_raw = [
-            sb.tile([P, PACK, CHUNK], F32, name="q_raw0", tag="queries_then_scales", align_bytes=256),
-            held.tile([P, PACK, CHUNK], F32, name="q_raw1", offset=0, align_bytes=256),
-            sb.tile([P, PACK, CHUNK], F32, name="q_raw2", align_bytes=256),
-            held.tile([P, PACK, CHUNK], F32, name="q_raw3", offset=4096, align_bytes=256),
+            sb.tile([P, PACK, CHUNK], F32, name="q_raw0", align_bytes=ALIGN),
+            held.tile([P, PACK, CHUNK], F32, name="q_raw1", offset=0, align_bytes=ALIGN),
+            sb.tile([P, PACK, CHUNK], F32, name="q_raw2", align_bytes=ALIGN),
+            held.tile([P, PACK, CHUNK], F32, name="q_raw3", offset=4096, align_bytes=ALIGN),
         ]
         nc.sync.dma_start(q_raw[0][:], q_rows[:, :, 0:CHUNK])
 
-        ks = sb.tile([P, T], U8, name="ks", align_bytes=256)
+        ks = sb.tile([P, T], U8, name="ks", align_bytes=ALIGN)
         nc.vector.memset(ks[:].bitcast(I32), 0)
         for j in range(4):
             nc.sync.dma_start(ks[j:P:32, :].bitcast(I32), k_scales[0, j:16:4, :].bitcast(I32))
+        ident = sb.tile([P, P], F32, name="ident", align_bytes=ALIGN)
+        nc.vector.memset(ident[:], 0.0)
+        make_identity(nc, ident[:], nomemset=True)
         nc.vector.memset(nbt[0:BIAS_ROW, :], 0.0)
 
-        kw = sb.tile([P, T], I32, name="kw", align_bytes=256)
+        kw = sb.tile([P, T], I32, name="kw", align_bytes=ALIGN)
         nc.sync.dma_start(kw[:], k_words[0].rearrange("p t r -> p (t r)").bitcast(I32))
         for c in range(1, n_chunks):
             nc.sync.dma_start(q_raw[c][:], q_rows[:, :, c * CHUNK : (c + 1) * CHUNK])
 
-        ident = sb.tile([P, P], F32, name="ident", align_bytes=256)
-        nc.vector.memset(ident[:], 0.0)
-        make_identity(nc, ident[:], nomemset=True)
+        q_bf0 = sb.tile([P, CHUNK * PACK], BF16, name="q_bf0", align_bytes=ALIGN)
+        nc.scalar.copy(woven(q_bf0[:, 0 : SCALAR_SHARE * PACK]), planar(q_raw[0][:, :, 0:SCALAR_SHARE]))
 
-        nbg = sb.tile([P, N], F32, name="nbg", align_bytes=256)
-        nc.vector.tensor_copy(nbg[:], nbt[:].indirect(offsets[:]))
-        ksg = sb.tile([P, N], U8, name="ksg", align_bytes=256)
-        nc.vector.tensor_copy(ksg[:], ks[:].indirect(offsets[:]))
+        nbg = sb.tile([P, N], F32, name="nbg", align_bytes=ALIGN)
+        nc.scalar.activation(nbg[:], nbt[:].indirect(offsets[:]), COPY)
         bias_ps = ps.tile([P, PACK, P], F32, name="bias_ps", tag="bank7")
         for r in range(PACK):
             nc.tensor.transpose(bias_ps[:, r, :], nbg[:, r::PACK], ident[:])
-        bias = sb.tile([P, PACK], F32, name="bias", align_bytes=256)
+        bias = sb.tile([P, PACK], F32, name="bias", align_bytes=ALIGN)
         nc.scalar.copy(bias[:], bias_ps[:, :, BIAS_ROW])
 
-        y_codes = sb.tile([P, NQ], I32, name="y_codes", align_bytes=256)
-        y_scales = sb.tile([P, NQ], U8, name="y_scales", align_bytes=256)
+        y_codes = sb.tile([P, NQ], I32, name="y_codes", align_bytes=ALIGN)
+        y_scales = sb.tile([P, NQ], U8, name="y_scales", align_bytes=ALIGN)
         y_rows = out_0.rearrange("(p r) q -> p r q", r=PACK)
         y_words = out_1[0].rearrange("p q u -> p (q u)").bitcast(I32)
 
+        ksg = sb.tile([P, N], U8, name="ksg", align_bytes=ALIGN)
+        kg = sb.tile([P, N], U32, name="kg", align_bytes=ALIGN)
         q_codes, q_scales = [], []
         for c in range(n_chunks):
-            if c == 2:
-                q_bf = held.tile([P, CHUNK * PACK], BF16, name="q_bf2", offset=0, align_bytes=256)
+            if c == 0:
+                q_bf = q_bf0
+            elif c == 2:
+                q_bf = held.tile([P, CHUNK * PACK], BF16, name="q_bf2", offset=0, align_bytes=ALIGN)
             else:
-                q_bf = sb.tile([P, CHUNK * PACK], BF16, name=f"q_bf{c}", align_bytes=256)
-            if c < 2:
+                q_bf = sb.tile([P, CHUNK * PACK], BF16, name=f"q_bf{c}", align_bytes=ALIGN)
+            if c == 0:
+                nc.vector.tensor_copy(woven(q_bf[:, SCALAR_SHARE * PACK :]), planar(q_raw[c][:, :, SCALAR_SHARE:]))
+            elif c == 1:
                 nc.scalar.copy(woven(q_bf[:]), planar(q_raw[c][:]))
             else:
                 nc.vector.tensor_copy(woven(q_bf[:]), planar(q_raw[c][:]))
-            codes = sb.tile([P, CHUNK], U32, name=f"q_codes{c}", align_bytes=256)
-            scales = sb.tile([P, CHUNK], U8, name=f"q_scales{c}", align_bytes=256)
+            if c == 0:
+                nc.vector.tensor_copy(dealt(ksg[:]), ks[:].indirect(offsets[:]))
+            codes = sb.tile([P, CHUNK], U32, name=f"q_codes{c}", align_bytes=ALIGN)
+            scales = sb.tile([P, CHUNK], U8, name=f"q_scales{c}", align_bytes=ALIGN)
             nc.vector.quantize_mx(codes[:].bitcast(FP8X4), scales[:], q_bf[:])
             q_codes.append(codes)
             q_scales.append(scales)
             if c == 0:
-                ksd = sb.tile([P, N], U8, name="ksd", tag="queries_then_scales", align_bytes=256)
-                nc.vector.tensor_copy(
-                    ksd[:].rearrange("p (r c i) -> p c r i", r=PACK, i=16),
-                    ksg[:].rearrange("p (c i r) -> p c r i", r=PACK, i=16),
-                )
-                kg = sb.tile([P, N], U32, name="kg", align_bytes=256)
-                nc.vector.tensor_copy(
-                    kg[:].rearrange("p (r s) -> p s r", r=PACK),
-                    kw[:].bitcast(U32).indirect(offsets[:]),
-                )
+                nc.vector.tensor_copy(dealt(kg[:]), kw[:].bitcast(U32).indirect(offsets[:]))
 
         y_pair = [
-            held.tile([P, 2 * CHUNK * PACK], BF16, name="y_bf0", offset=5120, align_bytes=256),
-            sb.tile([P, 2 * CHUNK * PACK], BF16, name="y_bf1", align_bytes=256),
+            held.tile([P, 2 * CHUNK * PACK], BF16, name="y_bf0", offset=5120, align_bytes=ALIGN),
+            sb.tile([P, 2 * CHUNK * PACK], BF16, name="y_bf1", align_bytes=ALIGN),
         ]
         y = [
-            held.tile([P, PACK, CHUNK], F32, name="y0", offset=1024, align_bytes=256),
-            held.tile([P, PACK, CHUNK], F32, name="y1", offset=3072, align_bytes=256),
-            sb.tile([P, PACK, CHUNK], F32, name="y2", align_bytes=256),
-            sb.tile([P, PACK, CHUNK], F32, name="y3", align_bytes=256),
+            held.tile([P, PACK, CHUNK], F32, name="y0", offset=1024, align_bytes=ALIGN),
+            held.tile([P, PACK, CHUNK], F32, name="y1", offset=3072, align_bytes=ALIGN),
+            sb.tile([P, PACK, CHUNK], F32, name="y2", align_bytes=ALIGN),
+            sb.tile([P, PACK, CHUNK], F32, name="y3", align_bytes=ALIGN),
         ]
 
         def rounded(c):
@@ -138,7 +144,7 @@ def tile_attend_plh_brelu_topk_kernel(tc, qT, k_words, k_scales, nb, offs, out_0
                     nc.tensor.matmul_mx(
                         acc[:, u, :],
                         lhsT=kg[:, r * P : (r + 1) * P].bitcast(FP8X4),
-                        lhsT_scale=ksd[:, r * P : (r + 1) * P],
+                        lhsT_scale=ksg[:, r * P : (r + 1) * P],
                         rhs=q_codes[c][:].bitcast(FP8X4),
                         rhs_scale=q_scales[c][:],
                         start=True,

@@ -156,7 +156,11 @@ def tile_attend_plh_brelu_topk_kernel(tc, qT, k_words, k_scales, nb, offs, out_0
                         nc.vector.tensor_scalar(y[c][:, r, :], acc[:, u, :], bias[:, r : r + 1], 0.0, op0=ADD, op1=MAX)
                     else:
                         nc.scalar.activation(y[c][:, r, :], acc[:, u, :], RELU, bias=bias[:, r : r + 1])
-            nc.sync.dma_start(y_rows[:, :, c * CHUNK : (c + 1) * CHUNK], y[c][:])
+                if c < 2:
+                    rows = slice(2 * h, 2 * h + 2)
+                    nc.sync.dma_start(y_rows[:, rows, c * CHUNK : (c + 1) * CHUNK], y[c][:, rows, :])
+            if c >= 2:
+                nc.sync.dma_start(y_rows[:, :, c * CHUNK : (c + 1) * CHUNK], y[c][:])
 
         def weave(c):
             nc.vector.tensor_copy(woven(rounded(c)), planar(y[c][:]))

@@ -22,6 +22,8 @@ N = 512
 NQ = 512
 D = 512
 CHUNK = 128
+TEETH = 1
+TOOTH = CHUNK // TEETH
 BIAS_ROW = P - 1
 ALIGN = 256
 SCALAR_SHARE = 32
@@ -42,28 +44,52 @@ def dealt(tile):
     return tile.rearrange("p (r s) -> p s r", r=PACK)
 
 
+def planes(flat):
+    return flat.rearrange("p (t q) -> p t q", t=PACK)
+
+
+def comb(rows, c):
+    return rows.rearrange("(p t) (h x) -> p (t h) x", t=PACK, h=TEETH)[:, :, c * TOOTH : (c + 1) * TOOTH]
+
+
+def teeth(flat):
+    return flat.rearrange("p (g x) -> p g x", x=TOOTH)
+
+
 def tile_attend_plh_brelu_topk_kernel(tc, qT, k_words, k_scales, nb, offs, out_0, out_1, out_2):
     nc = tc.nc
     with ExitStack() as ctx:
         sb = ctx.enter_context(tc.tile_pool(name="sb", bufs=1))
-        held = ctx.enter_context(tc.tile_pool(name="held", bufs=1))
         ps = ctx.enter_context(tc.psum_pool(name="ps", bufs=1))
         n_chunks = NQ // CHUNK
         last = n_chunks - 1
+        width = PACK * CHUNK
 
         offsets = sb.tile([P, N // 16], U16, name="offsets", align_bytes=ALIGN)
         nc.sync.dma_start(offsets[:], offs)
         nbt = sb.tile([P, T], F32, name="nbt", align_bytes=ALIGN)
         nc.scalar.dma_start(nbt[BIAS_ROW:P, :], nb[0:1, :])
 
-        q_rows = qT[0].rearrange("(p j) q -> p j q", j=PACK)
-        q_raw = [
-            sb.tile([P, PACK, CHUNK], F32, name="q_raw0", align_bytes=ALIGN),
-            held.tile([P, PACK, CHUNK], F32, name="q_raw1", offset=0, align_bytes=ALIGN),
-            sb.tile([P, PACK, CHUNK], F32, name="q_raw2", align_bytes=ALIGN),
-            held.tile([P, PACK, CHUNK], F32, name="q_raw3", offset=4096, align_bytes=ALIGN),
+        shared1 = sb.tile([P, 10 * CHUNK], F32, name="shared1", align_bytes=ALIGN)
+        shared2 = sb.tile([P, width], F32, name="shared2", align_bytes=ALIGN)
+        shared3 = sb.tile([P, width], F32, name="shared3", align_bytes=ALIGN)
+        q_raw0 = sb.tile([P, width], F32, name="q_raw0", align_bytes=ALIGN)
+        q_bf0 = sb.tile([P, width], BF16, name="q_bf0", align_bytes=ALIGN)
+        y2 = sb.tile([P, width], F32, name="y2", align_bytes=ALIGN)
+        y3 = sb.tile([P, width], F32, name="y3", align_bytes=ALIGN)
+        y_bf_late = sb.tile([P, 3 * width], BF16, name="y_bf_late", align_bytes=ALIGN)
+        q_raw = [q_raw0[:], shared1[:, 3 * CHUNK : 7 * CHUNK], shared2[:], shared3[:]]
+        q_bf = [
+            q_bf0[:],
+            shared1[:, 8 * CHUNK : 10 * CHUNK].bitcast(BF16),
+            shared1[:, 3 * CHUNK : 5 * CHUNK].bitcast(BF16),
+            shared2[:, 0 : 2 * CHUNK].bitcast(BF16),
         ]
-        nc.sync.dma_start(q_raw[0][:], q_rows[:, :, 0:CHUNK])
+        y = [shared1[:, 5 * CHUNK : 9 * CHUNK], shared1[:, 0 : 4 * CHUNK], y2[:], y3[:]]
+        y_bf = [shared3[:, 0 : 2 * CHUNK].bitcast(BF16)]
+        y_bf.extend(y_bf_late[:, c * width : (c + 1) * width] for c in range(last))
+
+        nc.sync.dma_start(teeth(q_raw[0]), comb(qT[0], 0))
 
         ks = sb.tile([P, T], U8, name="ks", align_bytes=ALIGN)
         nc.vector.memset(ks[:].bitcast(I32), 0)
@@ -77,10 +103,9 @@ def tile_attend_plh_brelu_topk_kernel(tc, qT, k_words, k_scales, nb, offs, out_0
         kw = sb.tile([P, T], I32, name="kw", align_bytes=ALIGN)
         nc.sync.dma_start(kw[:], k_words[0].rearrange("p t r -> p (t r)").bitcast(I32))
         for c in range(1, n_chunks):
-            nc.sync.dma_start(q_raw[c][:], q_rows[:, :, c * CHUNK : (c + 1) * CHUNK])
+            nc.sync.dma_start(teeth(q_raw[c]), comb(qT[0], c))
 
-        q_bf0 = sb.tile([P, CHUNK * PACK], BF16, name="q_bf0", align_bytes=ALIGN)
-        nc.scalar.copy(woven(q_bf0[:, 0 : SCALAR_SHARE * PACK]), planar(q_raw[0][:, :, 0:SCALAR_SHARE]))
+        nc.scalar.copy(woven(q_bf[0][:, 0 : SCALAR_SHARE * PACK]), planar(planes(q_raw[0])[:, :, 0:SCALAR_SHARE]))
 
         nbg = sb.tile([P, N], F32, name="nbg", align_bytes=ALIGN)
         nc.scalar.activation(nbg[:], nbt[:].indirect(offsets[:]), COPY)
@@ -92,99 +117,110 @@ def tile_attend_plh_brelu_topk_kernel(tc, qT, k_words, k_scales, nb, offs, out_0
 
         y_codes = sb.tile([P, NQ], I32, name="y_codes", align_bytes=ALIGN)
         y_scales = sb.tile([P, NQ], U8, name="y_scales", align_bytes=ALIGN)
-        y_rows = out_0.rearrange("(p r) q -> p r q", r=PACK)
         y_words = out_1[0].rearrange("p q u -> p (q u)").bitcast(I32)
-
         ksg = sb.tile([P, N], U8, name="ksg", align_bytes=ALIGN)
         kg = sb.tile([P, N], U32, name="kg", align_bytes=ALIGN)
-        q_codes, q_scales = [], []
-        for c in range(n_chunks):
-            if c == 0:
-                q_bf = q_bf0
-            elif c == 2:
-                q_bf = held.tile([P, CHUNK * PACK], BF16, name="q_bf2", offset=0, align_bytes=ALIGN)
-            else:
-                q_bf = sb.tile([P, CHUNK * PACK], BF16, name=f"q_bf{c}", align_bytes=ALIGN)
-            if c == 0:
-                nc.vector.tensor_copy(woven(q_bf[:, SCALAR_SHARE * PACK :]), planar(q_raw[c][:, :, SCALAR_SHARE:]))
-            elif c == 1:
-                nc.scalar.copy(woven(q_bf[:]), planar(q_raw[c][:]))
-            else:
-                nc.vector.tensor_copy(woven(q_bf[:]), planar(q_raw[c][:]))
-            if c == 0:
-                nc.vector.tensor_copy(dealt(ksg[:]), ks[:].indirect(offsets[:]))
-            codes = sb.tile([P, CHUNK], U32, name=f"q_codes{c}", align_bytes=ALIGN)
-            scales = sb.tile([P, CHUNK], U8, name=f"q_scales{c}", align_bytes=ALIGN)
-            nc.vector.quantize_mx(codes[:].bitcast(FP8X4), scales[:], q_bf[:])
-            q_codes.append(codes)
-            q_scales.append(scales)
-            if c == 0:
-                nc.vector.tensor_copy(dealt(kg[:]), kw[:].bitcast(U32).indirect(offsets[:]))
+        q_codes = [sb.tile([P, CHUNK], U32, name=f"q_codes{c}", align_bytes=ALIGN) for c in range(n_chunks)]
+        q_scales = [sb.tile([P, CHUNK], U8, name=f"q_scales{c}", align_bytes=ALIGN) for c in range(n_chunks)]
+        sums = {}
 
-        y_pair = [
-            held.tile([P, 2 * CHUNK * PACK], BF16, name="y_bf0", offset=5120, align_bytes=ALIGN),
-            sb.tile([P, 2 * CHUNK * PACK], BF16, name="y_bf1", align_bytes=ALIGN),
-        ]
-        y = [
-            held.tile([P, PACK, CHUNK], F32, name="y0", offset=1024, align_bytes=ALIGN),
-            held.tile([P, PACK, CHUNK], F32, name="y1", offset=3072, align_bytes=ALIGN),
-            sb.tile([P, PACK, CHUNK], F32, name="y2", align_bytes=ALIGN),
-            sb.tile([P, PACK, CHUNK], F32, name="y3", align_bytes=ALIGN),
-        ]
+        def round_queries(c):
+            nc.vector.tensor_copy(woven(q_bf[c]), planar(planes(q_raw[c])))
 
-        def rounded(c):
-            return y_pair[c // 2][:, (c % 2) * CHUNK * PACK : (c % 2 + 1) * CHUNK * PACK]
+        def quantise_queries(c):
+            nc.vector.quantize_mx(q_codes[c][:].bitcast(FP8X4), q_scales[c][:], q_bf[c])
 
-        def multiply(c):
-            for h in range(PACK // 2):
-                bank = (PACK // 2) * c + h
-                acc = ps.tile([P, 2, CHUNK], F32, name=f"acc{bank}", tag=f"bank{bank}")
-                for u in range(2):
-                    r = 2 * h + u
-                    nc.tensor.matmul_mx(
-                        acc[:, u, :],
-                        lhsT=kg[:, r * P : (r + 1) * P].bitcast(FP8X4),
-                        lhsT_scale=ksg[:, r * P : (r + 1) * P],
-                        rhs=q_codes[c][:].bitcast(FP8X4),
-                        rhs_scale=q_scales[c][:],
-                        start=True,
-                        stop=True,
-                    )
-                for u in range(2):
-                    r = 2 * h + u
-                    if c == 1 and h == 1:
-                        nc.vector.tensor_scalar(y[c][:, r, :], acc[:, u, :], bias[:, r : r + 1], 0.0, op0=ADD, op1=MAX)
-                    else:
-                        nc.scalar.activation(y[c][:, r, :], acc[:, u, :], RELU, bias=bias[:, r : r + 1])
-                if c < 2:
-                    rows = slice(2 * h, 2 * h + 2)
-                    nc.sync.dma_start(y_rows[:, rows, c * CHUNK : (c + 1) * CHUNK], y[c][:, rows, :])
-            if c >= 2:
-                nc.sync.dma_start(y_rows[:, :, c * CHUNK : (c + 1) * CHUNK], y[c][:])
+        def multiply(c, rows, bank):
+            acc = ps.tile([P, len(rows), CHUNK], F32, name=f"acc{c}_{rows[0]}", tag=f"bank{bank}")
+            for u, r in enumerate(rows):
+                nc.tensor.matmul_mx(
+                    acc[:, u, :],
+                    lhsT=kg[:, r * P : (r + 1) * P].bitcast(FP8X4),
+                    lhsT_scale=ksg[:, r * P : (r + 1) * P],
+                    rhs=q_codes[c][:].bitcast(FP8X4),
+                    rhs_scale=q_scales[c][:],
+                    start=True,
+                    stop=True,
+                )
+                sums[(c, r)] = acc[:, u, :]
+
+        def relu_on_scalar(c, rows):
+            for r in rows:
+                nc.scalar.activation(planes(y[c])[:, r, :], sums[(c, r)], RELU, bias=bias[:, r : r + 1])
+
+        def relu_on_vector(c, r):
+            nc.vector.tensor_scalar(planes(y[c])[:, r, :], sums[(c, r)], bias[:, r : r + 1], 0.0, op0=ADD, op1=MAX)
+
+        def store(c, first, count):
+            runs = slice(TEETH * first, TEETH * (first + count))
+            nc.sync.dma_start(comb(out_0, c)[:, runs, :], teeth(y[c])[:, runs, :])
 
         def weave(c):
-            nc.vector.tensor_copy(woven(rounded(c)), planar(y[c][:]))
+            nc.vector.tensor_copy(woven(y_bf[c]), planar(planes(y[c])))
 
-        def quantise(c):
-            cols = slice(c * CHUNK, (c + 1) * CHUNK)
-            nc.vector.quantize_mx(y_codes[:, cols].bitcast(FP8X4), y_scales[:, cols], rounded(c))
-            if c % 2 == 1:
-                pair = slice((c - 1) * CHUNK, (c + 1) * CHUNK)
-                nc.sync.dma_start(y_words[:, pair], y_codes[:, pair])
+        def quantise_results(c):
+            for h in range(TEETH):
+                cols = slice(h * NQ // TEETH + c * TOOTH, h * NQ // TEETH + (c + 1) * TOOTH)
+                source = y_bf[c][:, h * TOOTH * PACK : (h + 1) * TOOTH * PACK]
+                nc.vector.quantize_mx(y_codes[:, cols].bitcast(FP8X4), y_scales[:, cols], source)
 
-        multiply(0)
-        multiply(1)
+        def store_codes(pair):
+            cols = slice(pair * 2 * TOOTH, (pair + 1) * 2 * TOOTH)
+            nc.sync.dma_start(
+                y_words.rearrange("p (h x) -> p h x", h=TEETH)[:, :, cols],
+                y_codes[:].rearrange("p (h x) -> p h x", h=TEETH)[:, :, cols],
+            )
+
+        nc.vector.tensor_copy(
+            woven(q_bf[0][:, SCALAR_SHARE * PACK :]), planar(planes(q_raw[0])[:, :, SCALAR_SHARE:])
+        )
+        nc.vector.tensor_copy(dealt(ksg[:]), ks[:].indirect(offsets[:]))
+        quantise_queries(0)
+        nc.vector.tensor_copy(dealt(kg[:]), kw[:].bitcast(U32).indirect(offsets[:]))
+        nc.scalar.copy(woven(q_bf[1]), planar(planes(q_raw[1])))
+        quantise_queries(1)
+
+        multiply(0, (0, 1), 0)
+        multiply(0, (3,), 1)
+        multiply(0, (2,), 2)
+        relu_on_scalar(0, (0, 1))
+        store(0, 0, 2)
+        round_queries(2)
+        relu_on_vector(0, 3)
+        quantise_queries(2)
+        relu_on_scalar(0, (2,))
+        store(0, 2, 2)
+
+        multiply(1, (0, 1), 3)
+        multiply(1, (2,), 4)
+        multiply(1, (3,), 5)
+        relu_on_scalar(1, (0, 1))
+        store(1, 0, 2)
+        round_queries(3)
+        relu_on_vector(1, 3)
+        quantise_queries(3)
+        relu_on_scalar(1, (2,))
+        store(1, 2, 2)
+
         weave(0)
         weave(1)
-        quantise(0)
-        multiply(2)
-        quantise(1)
+        multiply(2, (0, 1), 6)
+        multiply(2, (2, 3), 7)
+        relu_on_scalar(2, range(PACK))
+        store(2, 0, PACK)
+        quantise_results(0)
+        quantise_results(1)
+        store_codes(0)
         weave(2)
-        multiply(3)
-        nc.vector.tensor_copy(woven(rounded(last))[:, :, 0:2, :], planar(y[last][:, 0:2, :]))
-        nc.vector.tensor_copy(woven(rounded(last))[:, :, 2:4, :], planar(y[last][:, 2:4, :]))
-        quantise(2)
-        quantise(3)
+        multiply(3, (0, 1), 0)
+        multiply(3, (2, 3), 1)
+        relu_on_scalar(3, range(PACK))
+        store(3, 0, PACK)
+        nc.vector.tensor_copy(woven(y_bf[last])[:, :, 0:2, :], planar(planes(y[last])[:, 0:2, :]))
+        nc.vector.tensor_copy(woven(y_bf[last])[:, :, 2:4, :], planar(planes(y[last])[:, 2:4, :]))
+        quantise_results(2)
+        quantise_results(3)
+        store_codes(1)
         for j in range(4):
             queue = nc.sync if j % 2 == 0 else nc.scalar
             queue.dma_start(out_2[0, j:16:4, :].bitcast(I32), y_scales[j:P:32, :].bitcast(I32))

@@ -60,6 +60,7 @@ def tile_attend_plh_brelu_topk_kernel(tc, qT, k_words, k_scales, nb, offs, out_0
     nc = tc.nc
     with ExitStack() as ctx:
         sb = ctx.enter_context(tc.tile_pool(name="sb", bufs=1))
+        held = ctx.enter_context(tc.tile_pool(name="held", bufs=1))
         ps = ctx.enter_context(tc.psum_pool(name="ps", bufs=1))
         n_chunks = NQ // CHUNK
         last = n_chunks - 1
@@ -70,24 +71,24 @@ def tile_attend_plh_brelu_topk_kernel(tc, qT, k_words, k_scales, nb, offs, out_0
         nbt = sb.tile([P, T], F32, name="nbt", align_bytes=ALIGN)
         nc.scalar.dma_start(nbt[BIAS_ROW:P, :], nb[0:1, :])
 
-        shared1 = sb.tile([P, 10 * CHUNK], F32, name="shared1", align_bytes=ALIGN)
+        shared1 = sb.tile([P, 7 * CHUNK], F32, name="shared1", align_bytes=ALIGN)
         shared2 = sb.tile([P, width], F32, name="shared2", align_bytes=ALIGN)
-        shared3 = sb.tile([P, width], F32, name="shared3", align_bytes=ALIGN)
+        shared3 = sb.tile([P, 7 * CHUNK], F32, name="shared3", align_bytes=ALIGN)
         q_raw0 = sb.tile([P, width], F32, name="q_raw0", align_bytes=ALIGN)
         q_bf0 = sb.tile([P, width], BF16, name="q_bf0", align_bytes=ALIGN)
+        q_bf1 = sb.tile([P, width], BF16, name="q_bf1", align_bytes=ALIGN)
         y2 = sb.tile([P, width], F32, name="y2", align_bytes=ALIGN)
         y3 = sb.tile([P, width], F32, name="y3", align_bytes=ALIGN)
-        y_bf_late = sb.tile([P, 3 * width], BF16, name="y_bf_late", align_bytes=ALIGN)
-        q_raw = [q_raw0[:], shared1[:, 3 * CHUNK : 7 * CHUNK], shared2[:], shared3[:]]
+        q_raw = [q_raw0[:], shared1[:, 0 : 4 * CHUNK], shared2[:], shared3[:, 3 * CHUNK : 7 * CHUNK]]
         q_bf = [
             q_bf0[:],
-            shared1[:, 8 * CHUNK : 10 * CHUNK].bitcast(BF16),
-            shared1[:, 3 * CHUNK : 5 * CHUNK].bitcast(BF16),
+            q_bf1[:],
+            shared1[:, 5 * CHUNK : 7 * CHUNK].bitcast(BF16),
             shared2[:, 0 : 2 * CHUNK].bitcast(BF16),
         ]
-        y = [shared1[:, 5 * CHUNK : 9 * CHUNK], shared1[:, 0 : 4 * CHUNK], y2[:], y3[:]]
-        y_bf = [shared3[:, 0 : 2 * CHUNK].bitcast(BF16)]
-        y_bf.extend(y_bf_late[:, c * width : (c + 1) * width] for c in range(last))
+        y = [shared1[:, 2 * CHUNK : 6 * CHUNK], shared3[:, 0 : 4 * CHUNK], y2[:], y3[:]]
+        y_bf1 = sb.tile([P, width], BF16, name="y_bf1", align_bytes=ALIGN)
+        y_bf3 = sb.tile([P, width], BF16, name="y_bf3", align_bytes=ALIGN)
 
         nc.sync.dma_start(teeth(q_raw[0]), comb(qT[0], 0))
 
@@ -120,7 +121,10 @@ def tile_attend_plh_brelu_topk_kernel(tc, qT, k_words, k_scales, nb, offs, out_0
         y_words = out_1[0].rearrange("p q u -> p (q u)").bitcast(I32)
         ksg = sb.tile([P, N], U8, name="ksg", align_bytes=ALIGN)
         kg = sb.tile([P, N], U32, name="kg", align_bytes=ALIGN)
-        q_codes = [sb.tile([P, CHUNK], U32, name=f"q_codes{c}", align_bytes=ALIGN) for c in range(n_chunks)]
+        q_codes = [sb.tile([P, CHUNK], U32, name=f"q_codes{c}", align_bytes=ALIGN) for c in range(last)]
+        q_codes.append(held.tile([P, CHUNK], U32, name="q_codes3", offset=0, align_bytes=ALIGN))
+        y_bf2 = held.tile([P, width], BF16, name="y_bf2", offset=0, align_bytes=ALIGN)
+        y_bf = [shared3[:, 5 * CHUNK : 7 * CHUNK].bitcast(BF16), y_bf1[:], y_bf2[:], y_bf3[:]]
         q_scales = [sb.tile([P, CHUNK], U8, name=f"q_scales{c}", align_bytes=ALIGN) for c in range(n_chunks)]
         sums = {}
 
@@ -178,46 +182,46 @@ def tile_attend_plh_brelu_topk_kernel(tc, qT, k_words, k_scales, nb, offs, out_0
         quantise_queries(0)
         nc.vector.tensor_copy(dealt(kg[:]), kw[:].bitcast(U32).indirect(offsets[:]))
         nc.scalar.copy(woven(q_bf[1]), planar(planes(q_raw[1])))
+        round_queries(2)
         quantise_queries(1)
+        quantise_queries(2)
+        round_queries(3)
 
         multiply(0, (0, 1), 0)
         multiply(0, (3,), 1)
         multiply(0, (2,), 2)
         relu_on_scalar(0, (0, 1))
         store(0, 0, 2)
-        round_queries(2)
         relu_on_vector(0, 3)
-        quantise_queries(2)
+        quantise_queries(3)
         relu_on_scalar(0, (2,))
         store(0, 2, 2)
 
-        multiply(1, (0, 1), 3)
-        multiply(1, (2,), 4)
-        multiply(1, (3,), 5)
+        for r in range(PACK):
+            multiply(1, (r,), 3 + r)
         relu_on_scalar(1, (0, 1))
         store(1, 0, 2)
-        round_queries(3)
         relu_on_vector(1, 3)
-        quantise_queries(3)
         relu_on_scalar(1, (2,))
         store(1, 2, 2)
 
         weave(0)
         weave(1)
-        multiply(2, (0, 1), 6)
-        multiply(2, (2, 3), 7)
+        multiply(2, (0, 1), 7)
+        multiply(2, (2, 3), 0)
         relu_on_scalar(2, range(PACK))
         store(2, 0, PACK)
         quantise_results(0)
         quantise_results(1)
         store_codes(0)
-        weave(2)
-        multiply(3, (0, 1), 0)
-        multiply(3, (2, 3), 1)
-        relu_on_scalar(3, range(PACK))
+        multiply(3, (0, 1), 1)
+        multiply(3, (2,), 2)
+        multiply(3, (3,), 3)
+        relu_on_scalar(3, (0, 1, 2))
+        relu_on_vector(3, 3)
         store(3, 0, PACK)
-        nc.vector.tensor_copy(woven(y_bf[last])[:, :, 0:2, :], planar(planes(y[last])[:, 0:2, :]))
-        nc.vector.tensor_copy(woven(y_bf[last])[:, :, 2:4, :], planar(planes(y[last])[:, 2:4, :]))
+        weave(2)
+        weave(3)
         quantise_results(2)
         quantise_results(3)
         store_codes(1)

@@ -71,7 +71,7 @@ def tile_attend_plh_brelu_topk_kernel(tc, qT, k_words, k_scales, nb, offs, out_0
         nbt = sb.tile([P, T], F32, name="nbt", align_bytes=ALIGN)
         nc.scalar.dma_start(nbt[BIAS_ROW:P, :], nb[0:1, :])
 
-        shared1 = sb.tile([P, 7 * CHUNK], F32, name="shared1", align_bytes=ALIGN)
+        shared1 = sb.tile([P, 6 * CHUNK], F32, name="shared1", align_bytes=ALIGN)
         shared2 = sb.tile([P, width], F32, name="shared2", align_bytes=ALIGN)
         shared3 = sb.tile([P, 7 * CHUNK], F32, name="shared3", align_bytes=ALIGN)
         q_raw0 = sb.tile([P, width], F32, name="q_raw0", align_bytes=ALIGN)
@@ -83,7 +83,7 @@ def tile_attend_plh_brelu_topk_kernel(tc, qT, k_words, k_scales, nb, offs, out_0
         q_bf = [
             q_bf0[:],
             q_bf1[:],
-            shared1[:, 5 * CHUNK : 7 * CHUNK].bitcast(BF16),
+            shared1[:, 0 : 2 * CHUNK].bitcast(BF16),
             shared2[:, 0 : 2 * CHUNK].bitcast(BF16),
         ]
         y = [shared1[:, 2 * CHUNK : 6 * CHUNK], shared3[:, 0 : 4 * CHUNK], y2[:], y3[:]]
@@ -182,23 +182,22 @@ def tile_attend_plh_brelu_topk_kernel(tc, qT, k_words, k_scales, nb, offs, out_0
         quantise_queries(0)
         nc.vector.tensor_copy(dealt(kg[:]), kw[:].bitcast(U32).indirect(offsets[:]))
         nc.scalar.copy(woven(q_bf[1]), planar(planes(q_raw[1])))
-        round_queries(2)
         quantise_queries(1)
-        quantise_queries(2)
-        round_queries(3)
+        for c in range(2, n_chunks):
+            round_queries(c)
+            quantise_queries(c)
 
-        multiply(0, (0, 1), 0)
-        multiply(0, (3,), 1)
-        multiply(0, (2,), 2)
+        multiply(0, (0,), 0)
+        multiply(0, (1,), 1)
+        multiply(0, (2, 3), 2)
         relu_on_scalar(0, (0, 1))
         store(0, 0, 2)
-        relu_on_vector(0, 3)
-        quantise_queries(3)
-        relu_on_scalar(0, (2,))
+        relu_on_scalar(0, (2, 3))
         store(0, 2, 2)
 
-        for r in range(PACK):
-            multiply(1, (r,), 3 + r)
+        multiply(1, (0, 1), 3)
+        multiply(1, (2,), 4)
+        multiply(1, (3,), 5)
         relu_on_scalar(1, (0, 1))
         store(1, 0, 2)
         relu_on_vector(1, 3)

from contextlib import ExitStack

import concourse.mybir as mybir
from concourse.masks import make_identity

F32 = mybir.dt.float32
BF16 = mybir.dt.bfloat16
I32 = mybir.dt.int32
U32 = mybir.dt.uint32
U16 = mybir.dt.uint16
U8 = mybir.dt.uint8
FP8X4 = mybir.dt.float8_e4m3fn_x4
RELU = mybir.ActivationFunctionType.Relu
COPY = mybir.ActivationFunctionType.Copy
ADD = mybir.AluOpType.add
MAX = mybir.AluOpType.max

P = 128
PACK = 4
T = 2048
N = 512
NQ = 512
D = 512
CHUNK = 128
TEETH = 1
TOOTH = CHUNK // TEETH
BIAS_ROW = P - 1
ALIGN = 256
SCALAR_SHARE = 32

FLOPS = 2 * N * NQ * D
BYTES = D * NQ * 4 + P * T * 4 + 16 * T + T * 4 + P * 32 * 2 + N * NQ * 4 + N * NQ + 16 * NQ


def woven(tile):
    return tile.rearrange("p (c i t) -> p c t i", t=PACK, i=4)


def planar(rows):
    return rows.rearrange("p t (c i) -> p c t i", i=4)


def dealt(tile):
    return tile.rearrange("p (r s) -> p s r", r=PACK)


def planes(flat):
    return flat.rearrange("p (t q) -> p t q", t=PACK)


def comb(rows, c):
    return rows.rearrange("(p t) (h x) -> p (t h) x", t=PACK, h=TEETH)[:, :, c * TOOTH : (c + 1) * TOOTH]


def teeth(flat):
    return flat.rearrange("p (g x) -> p g x", x=TOOTH)


def tile_attend_plh_brelu_topk_kernel(tc, qT, k_words, k_scales, nb, offs, out_0, out_1, out_2):
    nc = tc.nc
    with ExitStack() as ctx:
        sb = ctx.enter_context(tc.tile_pool(name="sb", bufs=1))
        held = ctx.enter_context(tc.tile_pool(name="held", bufs=1))
        ps = ctx.enter_context(tc.psum_pool(name="ps", bufs=1))
        n_chunks = NQ // CHUNK
        last = n_chunks - 1
        width = PACK * CHUNK

        offsets = sb.tile([P, N // 16], U16, name="offsets", align_bytes=ALIGN)
        nc.sync.dma_start(offsets[:], offs)
        nbt = sb.tile([P, T], F32, name="nbt", align_bytes=ALIGN)
        nc.scalar.dma_start(nbt[BIAS_ROW:P, :], nb[0:1, :])

        shared1 = sb.tile([P, 6 * CHUNK], F32, name="shared1", align_bytes=ALIGN)
        shared2 = sb.tile([P, width], F32, name="shared2", align_bytes=ALIGN)
        shared3 = sb.tile([P, 7 * CHUNK], F32, name="shared3", align_bytes=ALIGN)
        q_raw0 = sb.tile([P, width], F32, name="q_raw0", align_bytes=ALIGN)
        q_bf0 = sb.tile([P, width], BF16, name="q_bf0", align_bytes=ALIGN)
        q_bf1 = sb.tile([P, width], BF16, name="q_bf1", align_bytes=ALIGN)
        y2 = sb.tile([P, width], F32, name="y2", align_bytes=ALIGN)
        y3 = sb.tile([P, width], F32, name="y3", align_bytes=ALIGN)
        q_raw = [q_raw0[:], shared1[:, 0 : 4 * CHUNK], shared2[:], shared3[:, 3 * CHUNK : 7 * CHUNK]]
        q_bf = [
            q_bf0[:],
            q_bf1[:],
            shared1[:, 0 : 2 * CHUNK].bitcast(BF16),
            shared2[:, 0 : 2 * CHUNK].bitcast(BF16),
        ]
        y = [shared1[:, 2 * CHUNK : 6 * CHUNK], shared3[:, 0 : 4 * CHUNK], y2[:], y3[:]]
        y_bf1 = sb.tile([P, width], BF16, name="y_bf1", align_bytes=ALIGN)
        y_bf3 = sb.tile([P, width], BF16, name="y_bf3", align_bytes=ALIGN)

        nc.sync.dma_start(teeth(q_raw[0]), comb(qT[0], 0))

        ks = sb.tile([P, T], U8, name="ks", align_bytes=ALIGN)
        nc.vector.memset(ks[:].bitcast(I32), 0)
        for j in range(4):
            nc.sync.dma_start(ks[j:P:32, :].bitcast(I32), k_scales[0, j:16:4, :].bitcast(I32))
        ident = sb.tile([P, P], F32, name="ident", align_bytes=ALIGN)
        nc.vector.memset(ident[:], 0.0)
        make_identity(nc, ident[:], nomemset=True)
        nc.vector.memset(nbt[0:BIAS_ROW, :], 0.0)

        kw = sb.tile([P, T], I32, name="kw", align_bytes=ALIGN)
        nc.sync.dma_start(kw[:], k_words[0].rearrange("p t r -> p (t r)").bitcast(I32))
        for c in range(1, n_chunks):
            nc.sync.dma_start(teeth(q_raw[c]), comb(qT[0], c))

        nc.scalar.copy(woven(q_bf[0][:, 0 : SCALAR_SHARE * PACK]), planar(planes(q_raw[0])[:, :, 0:SCALAR_SHARE]))

        nbg = sb.tile([P, N], F32, name="nbg", align_bytes=ALIGN)
        nc.scalar.activation(nbg[:], nbt[:].indirect(offsets[:]), COPY)
        bias_ps = ps.tile([P, PACK, P], F32, name="bias_ps", tag="bank7")
        for r in range(PACK):
            nc.tensor.transpose(bias_ps[:, r, :], nbg[:, r::PACK], ident[:])
        bias = sb.tile([P, PACK], F32, name="bias", align_bytes=ALIGN)
        nc.scalar.copy(bias[:], bias_ps[:, :, BIAS_ROW])

        y_codes = sb.tile([P, NQ], I32, name="y_codes", align_bytes=ALIGN)
        y_scales = sb.tile([P, NQ], U8, name="y_scales", align_bytes=ALIGN)
        y_words = out_1[0].rearrange("p q u -> p (q u)").bitcast(I32)
        ksg = sb.tile([P, N], U8, name="ksg", align_bytes=ALIGN)
        kg = sb.tile([P, N], U32, name="kg", align_bytes=ALIGN)
        q_codes = [sb.tile([P, CHUNK], U32, name=f"q_codes{c}", align_bytes=ALIGN) for c in range(last)]
        q_codes.append(held.tile([P, CHUNK], U32, name="q_codes3", offset=0, align_bytes=ALIGN))
        y_bf2 = held.tile([P, width], BF16, name="y_bf2", offset=0, align_bytes=ALIGN)
        y_bf = [shared3[:, 5 * CHUNK : 7 * CHUNK].bitcast(BF16), y_bf1[:], y_bf2[:], y_bf3[:]]
        q_scales = [sb.tile([P, CHUNK], U8, name=f"q_scales{c}", align_bytes=ALIGN) for c in range(n_chunks)]
        sums = {}

        def round_queries(c):
            nc.vector.tensor_copy(woven(q_bf[c]), planar(planes(q_raw[c])))

        def quantise_queries(c):
            nc.vector.quantize_mx(q_codes[c][:].bitcast(FP8X4), q_scales[c][:], q_bf[c])

        def multiply(c, rows, bank):
            acc = ps.tile([P, len(rows), CHUNK], F32, name=f"acc{c}_{rows[0]}", tag=f"bank{bank}")
            for u, r in enumerate(rows):
                nc.tensor.matmul_mx(
                    acc[:, u, :],
                    lhsT=kg[:, r * P : (r + 1) * P].bitcast(FP8X4),
                    lhsT_scale=ksg[:, r * P : (r + 1) * P],
                    rhs=q_codes[c][:].bitcast(FP8X4),
                    rhs_scale=q_scales[c][:],
                    start=True,
                    stop=True,
                )
                sums[(c, r)] = acc[:, u, :]

        def relu_on_scalar(c, rows):
            for r in rows:
                nc.scalar.activation(planes(y[c])[:, r, :], sums[(c, r)], RELU, bias=bias[:, r : r + 1])

        def relu_on_vector(c, r):
            nc.vector.tensor_scalar(planes(y[c])[:, r, :], sums[(c, r)], bias[:, r : r + 1], 0.0, op0=ADD, op1=MAX)

        def store(c, first, count):
            runs = slice(TEETH * first, TEETH * (first + count))
            nc.sync.dma_start(comb(out_0, c)[:, runs, :], teeth(y[c])[:, runs, :])

        def weave(c):
            nc.vector.tensor_copy(woven(y_bf[c]), planar(planes(y[c])))

        def quantise_results(c):
            for h in range(TEETH):
                cols = slice(h * NQ // TEETH + c * TOOTH, h * NQ // TEETH + (c + 1) * TOOTH)
                source = y_bf[c][:, h * TOOTH * PACK : (h + 1) * TOOTH * PACK]
                nc.vector.quantize_mx(y_codes[:, cols].bitcast(FP8X4), y_scales[:, cols], source)

        def store_codes(pair):
            cols = slice(pair * 2 * TOOTH, (pair + 1) * 2 * TOOTH)
            nc.sync.dma_start(
                y_words.rearrange("p (h x) -> p h x", h=TEETH)[:, :, cols],
                y_codes[:].rearrange("p (h x) -> p h x", h=TEETH)[:, :, cols],
            )

        nc.vector.tensor_copy(
            woven(q_bf[0][:, SCALAR_SHARE * PACK :]), planar(planes(q_raw[0])[:, :, SCALAR_SHARE:])
        )
        nc.vector.tensor_copy(dealt(ksg[:]), ks[:].indirect(offsets[:]))
        quantise_queries(0)
        nc.vector.tensor_copy(dealt(kg[:]), kw[:].bitcast(U32).indirect(offsets[:]))
        nc.scalar.copy(woven(q_bf[1]), planar(planes(q_raw[1])))
        quantise_queries(1)
        for c in range(2, n_chunks):
            round_queries(c)
            quantise_queries(c)

        multiply(0, (0,), 0)
        multiply(0, (1,), 1)
        multiply(0, (2, 3), 2)
        relu_on_scalar(0, (0, 1))
        store(0, 0, 2)
        relu_on_scalar(0, (2, 3))
        store(0, 2, 2)

        multiply(1, (0, 1), 3)
        multiply(1, (2,), 4)
        multiply(1, (3,), 5)
        relu_on_scalar(1, (0, 1))
        store(1, 0, 2)
        relu_on_vector(1, 3)
        relu_on_scalar(1, (2,))
        store(1, 2, 2)

        weave(0)
        weave(1)
        multiply(2, (0, 1), 7)
        multiply(2, (2, 3), 0)
        relu_on_scalar(2, range(PACK))
        store(2, 0, PACK)
        quantise_results(0)
        quantise_results(1)
        store_codes(0)
        multiply(3, (0, 1), 1)
        multiply(3, (2,), 2)
        multiply(3, (3,), 3)
        relu_on_scalar(3, (0, 1, 2))
        relu_on_vector(3, 3)
        store(3, 0, PACK)
        weave(2)
        weave(3)
        quantise_results(2)
        quantise_results(3)
        store_codes(1)
        for j in range(4):
            queue = nc.sync if j % 2 == 0 else nc.scalar
            queue.dma_start(out_2[0, j:16:4, :].bitcast(I32), y_scales[j:P:32, :].bitcast(I32))
